import numpy as np
import ml_dtypes


def mxq(x, axis, fmt="e4m3"):
    dtype, down = {"e4m3": (ml_dtypes.float8_e4m3fn, 7), "e5m2": (ml_dtypes.float8_e5m2, 14)}[fmt]
    v = np.moveaxis(np.asarray(x, np.float32).astype(ml_dtypes.bfloat16).astype(np.float64), axis, -1)
    blocks = v.reshape(v.shape[:-1] + (-1, 32))
    amax = np.abs(blocks).max(-1, keepdims=True)
    byte = np.maximum(np.where(amax > 0, np.frexp(amax)[1] - 1 + 127, 0) - down, 1)
    scale = np.exp2(byte - 127.0)
    codes = (blocks / scale).astype(np.float32).astype(dtype).astype(np.float64)
    return np.moveaxis((codes * scale).reshape(v.shape), -1, axis)


WIDE = False


def mx_kscale(k):
    if not WIDE:
        return np.ones(k)
    levels = np.array([10, -10, 5, -5, 0])
    if k % 512:
        return np.exp2(np.random.permutation(np.resize(levels, k // 32))).repeat(32)
    a = np.empty((k // 512, 16))
    for p in range(k // 512):
        a[p, :8] = np.random.permutation(np.resize(levels, 8))
        for g in range(8):
            far = levels[np.abs(levels - a[p, g]) >= 10]
            a[p, g + 8] = far[np.random.randint(len(far))]
    return np.exp2(a.ravel()).repeat(32)


def f64(x):
    return np.asarray(x).astype(np.float64)


def striped(idx):
    return np.tile(idx.reshape(-1, 16).T, (8, 1)).astype(np.uint16)


def unstriped(offs):
    return offs[:16].T.reshape(-1).astype(np.int64)


def striped8(idx):
    return np.concatenate([x.reshape(-1, 16).T for x in idx]).astype(np.uint16)


def runs(offs, k):
    lists = np.stack([offs[16 * r : 16 * r + 16].T.reshape(-1) for r in range(8)]).astype(np.int64)
    return lists[np.arange(k) % 512 // 64]


def pack_weight(w):
    k, n = w.shape
    w = f64(np.asarray(w, np.float32).astype(ml_dtypes.bfloat16)).reshape(k // 32, 32, n)
    amax = np.abs(w).max(1)
    byte = np.clip(np.where(amax > 0, np.frexp(amax)[1] - 1 + 127 - 7, 1), 1, 254)
    scaled = (w * np.exp2(127.0 - byte)[:, None, :]).reshape(k, n).astype(np.float32)
    words = np.ascontiguousarray(scaled.reshape(k // 512, 128, 4, n).transpose(0, 1, 3, 2)).astype(ml_dtypes.float8_e4m3fn).view(np.uint8)
    return words, np.ascontiguousarray(byte.astype(np.uint8).reshape(k // 512, 16, n))


def unpack_weight(words, scales):
    g, p, n, _ = words.shape
    vals = np.ascontiguousarray(words).view(ml_dtypes.float8_e4m3fn).astype(np.float64) * np.repeat(np.exp2(scales.astype(np.float64) - 127.0), 8, axis=1)[..., None]
    return vals.transpose(0, 1, 3, 2).reshape(g * 512, n)


E2M1 = np.array([0.0, 0.5, 1.0, 1.5, 2.0, 3.0, 4.0, 6.0, -0.0, -0.5, -1.0, -1.5, -2.0, -3.0, -4.0, -6.0])


def pack_fp4(w):
    k, n = w.shape
    w = f64(np.asarray(w, np.float32).astype(ml_dtypes.bfloat16)).reshape(k // 32, 32, n)
    amax = np.abs(w).max(1)
    mant, ex = np.frexp(amax / 6.0)
    byte = np.clip(np.where(amax > 0, np.where(mant > 0.5, ex, ex - 1) + 127, 1), 1, 254)
    scaled = (w * np.exp2(127.0 - byte)[:, None, :]).reshape(k, n).astype(np.float32)
    c = np.ascontiguousarray(scaled.reshape(k // 512, 128, 4, n).transpose(0, 1, 3, 2)).astype(ml_dtypes.float4_e2m1fn).view(np.uint8) & 0xF
    words = (c[..., 0::2] | (c[..., 1::2] << 4)).reshape(k // 512, 128, 2 * n)
    return np.ascontiguousarray(words), np.ascontiguousarray(byte.astype(np.uint8).reshape(k // 512, 16, n))


def unpack_fp4(words, scales):
    g, _, n = scales.shape
    words = np.ascontiguousarray(words).reshape(g, 128, n, 2)
    nib = np.empty((g, 128, n, 4), np.uint8)
    nib[..., 0::2] = words & 0xF
    nib[..., 1::2] = words >> 4
    vals = E2M1[nib] * np.repeat(np.exp2(scales.astype(np.float64) - 127.0), 8, axis=1)[..., None]
    return vals.transpose(0, 1, 3, 2).reshape(g * 512, n)


def planes(y):
    n, m = y.shape
    v = y.astype(np.float32).astype(ml_dtypes.bfloat16).astype(np.float64).reshape(n // 32, 32, m)
    top = np.abs(v).max(1)
    byte = np.clip(np.where(top > 0, np.frexp(top)[1] - 1 + 127 - 7, 1), 1, 254)
    codes = (v * np.exp2(127.0 - byte)[:, None, :]).reshape(n, m).astype(np.float32).astype(ml_dtypes.float8_e4m3fn).view(np.uint8)
    words = codes.reshape(n // 512, 128, 4, m).transpose(0, 1, 3, 2)
    return np.ascontiguousarray(words), np.ascontiguousarray(byte.astype(np.uint8).reshape(n // 512, 16, m))


K, T, S, V, H = 512, 2048, 512, 512, 512


def setup_inputs():
    n = np.random.standard_normal
    s = mx_kscale(K)[:, None]
    u = mx_kscale(S)
    packed_xT = pack_weight(n((K, T)) * s)
    packed_w1 = pack_fp4(n((K, H)) / np.sqrt(K) / s)
    packed_w2 = pack_fp4(n((K, H)) / np.sqrt(K) / s)
    packed_w3 = pack_fp4(n((K, H)) / np.sqrt(K) / s)
    return {
        "x_words": packed_xT[0],
        "x_scales": packed_xT[1],
        "w1_words": packed_w1[0],
        "w1_scales": packed_w1[1],
        "w2_words": packed_w2[0],
        "w2_scales": packed_w2[1],
        "w3_words": packed_w3[0],
        "w3_scales": packed_w3[1],
        "ga": (np.random.uniform(0.5, 1.5, (H, 1)) * u[:, None]).astype(np.float32),
        "gb": (np.random.uniform(0.5, 1.5, (H, 1)) / u[:, None]).astype(np.float32),
        "offs": striped(np.random.permutation(T)[:S]),
        "two": striped(np.random.permutation(T)[:S]),
        "n1": striped8(np.stack([np.random.permutation(S) for _ in range(8)])),
        "n2": striped8(np.stack([np.random.permutation(S) for _ in range(8)])),
        "three": striped(np.random.permutation(T)[:V]),
        "n3": striped8(np.stack([np.random.permutation(V) for _ in range(8)])),
        "n4": striped8(np.stack([np.random.permutation(V) for _ in range(8)])),
        "n5": striped8(np.stack([np.random.permutation(V) for _ in range(8)])),
        "n6": striped8(np.stack([np.random.permutation(V) for _ in range(8)])),
        "n7": striped8(np.stack([np.random.permutation(V) for _ in range(8)])),
    }


def reference(x_words, x_scales, w1_words, w1_scales, w2_words, w2_scales, w3_words, w3_scales, ga, gb, offs, two, n1, n2, three, n3, n4, n5, n6, n7):
    xq = unpack_weight(x_words, x_scales)[:, unstriped(offs)]
    y = unpack_fp4(w1_words, w1_scales).T @ xq
    x_two = unpack_weight(x_words, x_scales)[:, unstriped(two)]
    d = unpack_fp4(w2_words, w2_scales).T @ x_two
    z = f64(ga) * (y[np.arange(H)[:, None], runs(n1, H)] - (np.tanh(d) * (d[np.arange(H)[:, None], runs(n2, H)])))
    x_three = unpack_weight(x_words, x_scales)[:, unstriped(three)]
    b = unpack_fp4(w3_words, w3_scales).T @ x_three
    sq = (b) ** 2
    z2 = f64(gb) * ((b[np.arange(H)[:, None], runs(n4, H)]) / (np.sqrt(sq + sq[np.arange(H)[:, None], runs(n3, H)] + 0.25)))
    s = 0.0625 * ((mxq(z, 0, "e4m3").T @ mxq(z2, 0, "e4m3")))
    b1 = s[np.arange(S)[:, None], runs(n5, S)]
    b2 = s[np.arange(S)[:, None], runs(n6, S)]
    b3 = s[np.arange(S)[:, None], runs(n7, S)]
    out_0 = np.maximum(np.maximum(b1, b2), b3) - (0.5 * (np.maximum(np.minimum(b1, b2), np.minimum(np.maximum(b1, b2), b3))))
    return (out_0,) + planes(out_0)

@@ -1,0 +1,257 @@
+from contextlib import ExitStack
+
+import concourse.mybir as mybir
+from concourse.masks import make_identity
+
+F32 = mybir.dt.float32
+BF16 = mybir.dt.bfloat16
+I32 = mybir.dt.int32
+U32 = mybir.dt.uint32
+U16 = mybir.dt.uint16
+U8 = mybir.dt.uint8
+FP8X4 = mybir.dt.float8_e4m3fn_x4
+FP4X4 = mybir.dt.float4_e2m1fn_x4
+ALU = mybir.AluOpType
+ACT = mybir.ActivationFunctionType
+
+P = 128
+T = 2048
+S = 512
+PACK = 4
+HALF = 256
+FLOPS = 4 * 2 * 512 * 512 * 512
+
+
+def tile_picked_twksoftbrmstop2_none_po_kernel(tc, x_words, x_scales, w1_words, w1_scales, w2_words, w2_scales, w3_words, w3_scales, ga, gb, offs, two, n1, n2, three, n3, n4, n5, n6, n7, out_0, out_1, out_2):
+    nc = tc.nc
+    with ExitStack() as ctx:
+        keep = ctx.enter_context(tc.tile_pool(name="keep", bufs=1))
+        psum = ctx.enter_context(tc.psum_pool(name="psum", bufs=1))
+
+        def sb(name, shape, dtype):
+            return keep.tile(shape, dtype, name=name, align_bytes=64)
+
+        def bank(k):
+            return psum.tile([P, S], F32, name="bank%d" % k, tag="bank%d" % k)
+
+        def load_list(name, src):
+            tile = keep.tile([P, S // 16], U16, name=name)
+            nc.sync.dma_start(tile[:], src)
+            return tile
+
+        def load_scale_rows(queue, dst, src):
+            for q in range(4):
+                queue.dma_start(dst[32 * q : 32 * q + 4, :], src[0][4 * q : 4 * q + 4, :].bitcast(I32))
+
+        xs = sb("xs", [P, T // 4], I32)
+        nc.vector.memset(xs[:], 0)
+        wsc = [sb("wsc%d" % i, [P, S // 4], I32) for i in range(3)]
+        for i in range(3):
+            nc.vector.memset(wsc[i][:], 0)
+        l_two = load_list("l_two", two)
+        load_scale_rows(nc.sync, xs, x_scales)
+        l_three = load_list("l_three", three)
+        l_offs = load_list("l_offs", offs)
+        xw = sb("xw", [P, T], I32)
+        nc.sync.dma_start(xw[:], x_words[0].rearrange("p n t -> p (n t)").bitcast(I32))
+
+        ww = [sb("ww%d" % i, [P, S // 2], I32) for i in range(3)]
+        w_words = [w2_words, w3_words, w1_words]
+        w_scales = [w2_scales, w3_scales, w1_scales]
+        grow = sb("grow", [P, P], F32)
+        nc.gpsimd.memset(grow[:], 0.0)
+        nc.gpsimd.dma_start(grow[0:4, :].rearrange("t (b r) -> t b r", r=8), ga.rearrange("(b t r) o -> t b (r o)", t=4, r=8))
+        nc.gpsimd.dma_start(grow[4:8, :].rearrange("t (b r) -> t b r", r=8), gb.rearrange("(b t r) o -> t b (r o)", t=4, r=8))
+        ident = sb("ident", [P, P], F32)
+        make_identity(nc, ident[:])
+        quarter = sb("quarter", [P, 1], F32)
+        nc.gpsimd.memset(quarter[:], 0.25)
+        for i in range(3):
+            nc.sync.dma_start(ww[i][:], w_words[i][0].bitcast(I32))
+            load_scale_rows(nc.sync, wsc[i], w_scales[i])
+        l2 = load_list("l2", n2)
+        l3 = load_list("l3", n3)
+        l1 = load_list("l1", n1)
+        l4 = load_list("l4", n4)
+        l7 = load_list("l7", n7)
+        l5 = load_list("l5", n5)
+        l6 = load_list("l6", n6)
+
+        gps = bank(7)
+        nc.tensor.transpose(gps[:, 0:P], grow[:], ident[:])
+        gcol = sb("gcol", [P, 8], F32)
+        nc.scalar.copy(gcol[:], gps[:, 0:8])
+
+        lists = [l_two, l_three, l_offs]
+        xs_g = [sb("xs_g%d" % i, [P, S], U8) for i in range(3)]
+        xw_g = [sb("xw_g%d" % i, [P, S], U32) for i in range(3)]
+        wwd = [sb("wwd%d" % i, [P, S // 2], I32) for i in range(3)]
+        wsd = [sb("wsd%d" % i, [P, S // 4], I32) for i in range(3)]
+        for i in range(3):
+            nc.vector.tensor_copy(xs_g[i][:], xs[:].bitcast(U8).indirect(lists[i][:]))
+        for i in range(3):
+            nc.vector.tensor_copy(xw_g[i][:], xw[:].bitcast(U32).indirect(lists[i][:]))
+            nc.vector.tensor_copy(wwd[i][:].rearrange("p (t b w) -> p t b w", t=4, w=4), ww[i][:].rearrange("p (b t w) -> p t b w", t=4, w=4))
+            nc.vector.tensor_copy(wsd[i][:].rearrange("p (t b w) -> p t b w", t=4, w=2), wsc[i][:].rearrange("p (b t w) -> p t b w", t=4, w=2))
+
+        def product(i, t, acc):
+            nc.tensor.matmul_mx(
+                out=acc[:],
+                lhsT=wwd[i][:, 64 * t : 64 * t + 64].bitcast(U8).bitcast(FP4X4),
+                lhsT_scale=wsd[i][:, 32 * t : 32 * t + 32].bitcast(U8),
+                rhs=xw_g[i][:].bitcast(FP8X4),
+                rhs_scale=xs_g[i][:],
+                start=True,
+                stop=True,
+            )
+
+        def planes(name):
+            return [sb("%s%d" % (name, t), [P, S], F32) for t in range(PACK)]
+
+        def look_up(out, window, lst, lo, n, other, op):
+            picked = window[:].indirect(lst[:, lo // 16 : (lo + n) // 16])
+            if other is None:
+                nc.vector.tensor_copy(out, picked)
+            else:
+                nc.vector.tensor_tensor(out, picked, other, op)
+
+        th, dg, sq, sq2, bg, yg = planes("th"), planes("dg"), planes("sq"), planes("sqc"), planes("bg"), planes("yg")
+        pr, rr = planes("pr"), planes("rr")
+        us = planes("us")
+        d_ps = [bank(t) for t in range(PACK)]
+        b_ps = [bank(4 + t) for t in range(PACK)]
+        for t in range(PACK):
+            product(0, t, d_ps[t])
+            nc.scalar.activation(th[t][:], d_ps[t][:], ACT.Tanh)
+            nc.scalar.activation(dg[t][:], d_ps[t][:], ACT.Copy, scale=gcol[:, t : t + 1])
+        for t in range(PACK):
+            product(1, t, b_ps[t])
+            nc.scalar.activation(sq[t][:], b_ps[t][:], ACT.Square)
+            nc.sync.dma_start(sq2[t][:], sq[t][:])
+        for t in range(PACK):
+            nc.scalar.activation(bg[t][:], b_ps[t][:], ACT.Copy, scale=gcol[:, 4 + t : 5 + t])
+        y_ps = [bank(t) for t in range(PACK)]
+        for t in range(PACK):
+            product(2, t, y_ps[t])
+            nc.scalar.activation(yg[t][:], y_ps[t][:], ACT.Copy, scale=gcol[:, t : t + 1])
+
+        for t in range(PACK):
+            for lo in (0, HALF):
+                look_up(pr[t][:, lo : lo + HALF], dg[t], l2, lo, HALF, th[t][:, lo : lo + HALF], ALU.mult)
+        for t in range(PACK):
+            for lo in (0, HALF):
+                look_up(us[t][:, lo : lo + HALF], sq[t], l3, lo, HALF, sq2[t][:, lo : lo + HALF], ALU.add)
+            nc.scalar.activation(rr[t][:], us[t][:], ACT.Abs_reciprocal_sqrt, bias=quarter[:])
+        z = sb("z", [P, PACK, S], F32)
+        for t in range(PACK):
+            for lo in (0, HALF):
+                look_up(z[:, t, lo : lo + HALF], yg[t], l1, lo, HALF, pr[t][:, lo : lo + HALF], ALU.subtract)
+        zb = sb("zb", [P, PACK * S], BF16)
+        nc.scalar.copy(zb[:].rearrange("p (e m t) -> p m e t", e=4, t=4), z[:].rearrange("p t (m e) -> p m e t", e=4))
+        zq = sb("zq", [P, S], U32)
+        zs = sb("zs", [P, S], U8)
+
+        z2_parts = [(0, 256), (256, 128), (384, 128)]
+        z2q = sb("z2q", [P, S], U32)
+        z2s = sb("z2s", [P, S], U8)
+        s_ps = [bank(4 + e) for e in range(PACK)]
+        sw = planes("sw")
+        for k, (lo, n) in enumerate(z2_parts):
+            z2 = sb("z2_%d" % k, [P, PACK, n], F32)
+            z2b = sb("z2b_%d" % k, [P, PACK * n], BF16)
+            for t in range(PACK):
+                look_up(z2[:, t, :], bg[t], l4, lo, n, rr[t][:, lo : lo + n], ALU.mult)
+            if k == 0:
+                nc.vector.quantize_mx(out=zq[:].bitcast(FP8X4), scales=zs[:], in_=zb[:])
+            dst = z2b[:].rearrange("p (c i t) -> p c t i", i=4, t=4)
+            src = z2[:].rearrange("p t (c i) -> p c t i", i=4)
+            if k == len(z2_parts) - 1:
+                nc.vector.tensor_copy(dst, src)
+            else:
+                nc.scalar.copy(dst, src)
+            nc.vector.quantize_mx(out=z2q[:, lo : lo + n].bitcast(FP8X4), scales=z2s[:, lo : lo + n], in_=z2b[:])
+            for e in range(PACK):
+                nc.tensor.matmul_mx(
+                    out=s_ps[e][:, lo : lo + n],
+                    lhsT=zq[:, P * e : P * e + P].bitcast(FP8X4),
+                    lhsT_scale=zs[:, P * e : P * e + P],
+                    rhs=z2q[:, lo : lo + n].bitcast(FP8X4),
+                    rhs_scale=z2s[:, lo : lo + n],
+                    start=True,
+                    stop=True,
+                )
+                nc.scalar.activation(sw[e][:, lo : lo + n], s_ps[e][:, lo : lo + n], ACT.Copy, scale=0.03125)
+
+        oq = sb("oq", [P, S], I32)
+        osc = sb("osc", [P, S], U8)
+        out_rows = out_0.rearrange("(p e) v -> p e v", e=4)
+        words_out = out_1[0].rearrange("p n t -> p (n t)").bitcast(I32)
+        parts = [(0, HALF), (HALF, HALF)]
+        st = []
+        for k, (lo, n) in enumerate(parts):
+            st.append({nm: sb("%s_%d" % (nm, k), [P, PACK, n], F32) for nm in ("c", "u", "au", "hi", "pp", "tt", "o")})
+
+        def pair(tile, a):
+            return tile[:, 2 * a : 2 * a + 2, :].rearrange("p e v -> p (e v)")
+
+        def first(k, e):
+            lo, n = parts[k]
+            look_up(st[k]["c"][:, e, :], sw[e], l7, lo, n, None, None)
+
+        def middle(k):
+            lo, n = parts[k]
+            s = st[k]
+            for e in range(PACK):
+                look_up(s["u"][:, e, :], sw[e], l5, lo, n, s["c"][:, e, :], ALU.subtract)
+                if e % 2 == 1:
+                    nc.scalar.activation(pair(s["au"], e // 2), pair(s["u"], e // 2), ACT.Abs)
+            for a in range(2):
+                nc.vector.scalar_tensor_tensor(pair(s["hi"], a), pair(s["u"], a), 0.0, pair(s["c"], a), ALU.max, ALU.add)
+            for e in range(PACK):
+                look_up(s["pp"][:, e, :], sw[e], l6, lo, n, s["hi"][:, e, :], ALU.subtract)
+
+        def last(k, step, a):
+            s = st[k]
+            if step == 0:
+                nc.vector.scalar_tensor_tensor(pair(s["tt"], a), pair(s["pp"], a), -1.0, pair(s["au"], a), ALU.mult, ALU.min)
+            elif step == 1:
+                nc.vector.scalar_tensor_tensor(pair(s["u"], a), pair(s["tt"], a), -2.0, pair(s["tt"], a), ALU.mult, ALU.max)
+            else:
+                nc.vector.tensor_tensor(pair(s["o"], a), pair(s["u"], a), pair(s["hi"], a), ALU.add)
+
+        def leave(k):
+            lo, n = parts[k]
+            o = st[k]["o"]
+            nc.sync.dma_start(out_rows[:, :, lo : lo + n], o[:])
+            ob = sb("ob_%d" % k, [P, PACK * n], BF16)
+            dst = ob[:].rearrange("p (c i t) -> p c t i", i=4, t=4)
+            src = o[:].rearrange("p t (c i) -> p c t i", i=4)
+            if k == len(parts) - 1:
+                nc.vector.tensor_copy(dst, src)
+            else:
+                nc.scalar.copy(dst, src)
+            return ob
+
+        def hand_on(k, ob):
+            lo, n = parts[k]
+            nc.vector.quantize_mx(out=oq[:, lo : lo + n].bitcast(U32).bitcast(FP8X4), scales=osc[:, lo : lo + n], in_=ob[:])
+            nc.scalar.dma_start(words_out[:, lo : lo + n], oq[:, lo : lo + n])
+
+        for e in range(PACK):
+            first(0, e)
+        middle(0)
+        for step in range(3):
+            for a in range(2):
+                last(0, step, a)
+            first(1, step)
+        first(1, 3)
+        ob0 = leave(0)
+        middle(1)
+        hand_on(0, ob0)
+        for step in range(3):
+            for a in range(2):
+                last(1, step, a)
+        hand_on(1, leave(1))
+        for q in range(4):
+            queue = nc.sync if q % 2 == 0 else nc.scalar
+            queue.dma_start(out_2[0][4 * q : 4 * q + 4, :].bitcast(I32), osc[32 * q : 32 * q + 4, :].bitcast(I32))

@@ -41,20 +41,11 @@ def tile_picked_twksoftbrmstop2_none_po_kernel(tc, x_words, x_scales, w1_words, 
 
         def load_scale_rows(queue, dst, src):
             for q in range(4):
-                queue.dma_start(dst[32 * q : 32 * q + 4, :], src[0][4 * q : 4 * q + 4, :].bitcast(I32))
+                rows = src[0][4 * q : 4 * q + 4, :].bitcast(I32)
+                queue.dma_start(dst[32 * q : 32 * q + 32, :], rows.unsqueeze(0).broadcast_to([8, 4, rows.shape[1]]))
 
         xs = sb("xs", [P, T // 4], I32)
-        nc.vector.memset(xs[:], 0)
         wsc = [sb("wsc%d" % i, [P, S // 4], I32) for i in range(3)]
-        for i in range(3):
-            nc.vector.memset(wsc[i][:], 0)
-        l_two = load_list("l_two", two)
-        load_scale_rows(nc.sync, xs, x_scales)
-        l_three = load_list("l_three", three)
-        l_offs = load_list("l_offs", offs)
-        xw = sb("xw", [P, T], I32)
-        nc.sync.dma_start(xw[:], x_words[0].rearrange("p n t -> p (n t)").bitcast(I32))
-
         ww = [sb("ww%d" % i, [P, S // 2], I32) for i in range(3)]
         w_words = [w2_words, w3_words, w1_words]
         w_scales = [w2_scales, w3_scales, w1_scales]
@@ -66,10 +57,20 @@ def tile_picked_twksoftbrmstop2_none_po_kernel(tc, x_words, x_scales, w1_words, 
         make_identity(nc, ident[:])
         quarter = sb("quarter", [P, 1], F32)
         nc.gpsimd.memset(quarter[:], 0.25)
-        for i in range(3):
-            nc.sync.dma_start(ww[i][:], w_words[i][0].bitcast(I32))
-            load_scale_rows(nc.sync, wsc[i], w_scales[i])
+        load_scale_rows(nc.gpsimd, wsc[2], w_scales[2])
+
+        xw = sb("xw", [P, T], I32)
+        l_two = load_list("l_two", two)
+        load_scale_rows(nc.sync, xs, x_scales)
+        nc.sync.dma_start(xw[:], x_words[0].rearrange("p n t -> p (n t)").bitcast(I32))
+        l_three = load_list("l_three", three)
+        l_offs = load_list("l_offs", offs)
+        load_scale_rows(nc.sync, wsc[0], w_scales[0])
+        nc.sync.dma_start(ww[0][:], w_words[0][0].bitcast(I32))
+        nc.sync.dma_start(ww[1][:], w_words[1][0].bitcast(I32))
+        load_scale_rows(nc.sync, wsc[1], w_scales[1])
         l2 = load_list("l2", n2)
+        nc.sync.dma_start(ww[2][:], w_words[2][0].bitcast(I32))
         l3 = load_list("l3", n3)
         l1 = load_list("l1", n1)
         l4 = load_list("l4", n4)
@@ -84,7 +85,8 @@ def tile_picked_twksoftbrmstop2_none_po_kernel(tc, x_words, x_scales, w1_words, 
 
         lists = [l_two, l_three, l_offs]
         xs_g = [sb("xs_g%d" % i, [P, S], U8) for i in range(3)]
-        xw_g = [sb("xw_g%d" % i, [P, S], U32) for i in range(3)]
+        xw_tags = ["xw_g0", "wsc0", "xw_g2"]
+        xw_g = [keep.tile([P, S], U32, name="xw_g%d" % i, tag=xw_tags[i], align_bytes=64) for i in range(3)]
         wwd = [sb("wwd%d" % i, [P, S // 2], I32) for i in range(3)]
         wsd = [sb("wsd%d" % i, [P, S // 4], I32) for i in range(3)]
         for i in range(3):
@@ -115,61 +117,74 @@ def tile_picked_twksoftbrmstop2_none_po_kernel(tc, x_words, x_scales, w1_words, 
             else:
                 nc.vector.tensor_tensor(out, picked, other, op)
 
-        th, dg, sq, sq2, bg, yg = planes("th"), planes("dg"), planes("sq"), planes("sqc"), planes("bg"), planes("yg")
-        pr, rr = planes("pr"), planes("rr")
-        us = planes("us")
+        def windows(name, tags):
+            return [keep.tile([P, 2 * S], F32, name="%s%d" % (name, t), tag=tags[t], align_bytes=64) for t in range(PACK)]
+
+        dg_w = windows("dg", ["dg0", "dg1", "dg2", "dg3"])
+        sq_w = windows("sq", ["sq0", "wsc1", "sq2", "wsc2"])
+        yg_w = windows("yg", ["yg0", "yg1", "yg2", "yg3"])
+        dg = [w[:, 0:S] for w in dg_w]
+        sq = [w[:, 0:S] for w in sq_w]
+        yg = [w[:, 0:S] for w in yg_w]
+        th_last = sb("th_last", [P, S], F32)
+        th = [dg_w[t + 1][:, S:] for t in range(PACK - 1)] + [th_last[:]]
+        nc.gpsimd.memset(dg_w[0][:, S:], 0.0)
+        us = [w[:, S:] for w in yg_w]
+        sq2, bg = planes("sqc"), planes("bg")
+        rr = planes("rr")
+        pr = [w[:, S:] for w in sq_w]
         d_ps = [bank(t) for t in range(PACK)]
         b_ps = [bank(4 + t) for t in range(PACK)]
-        for t in range(PACK):
+        def leave_d(t):
             product(0, t, d_ps[t])
-            nc.scalar.activation(th[t][:], d_ps[t][:], ACT.Tanh)
-            nc.scalar.activation(dg[t][:], d_ps[t][:], ACT.Copy, scale=gcol[:, t : t + 1])
-        for t in range(PACK):
+            nc.scalar.activation(th[t], d_ps[t][:], ACT.Tanh)
+            nc.scalar.activation(dg[t], d_ps[t][:], ACT.Copy, scale=gcol[:, t : t + 1])
+
+        def square_b(t):
             product(1, t, b_ps[t])
-            nc.scalar.activation(sq[t][:], b_ps[t][:], ACT.Square)
-            nc.sync.dma_start(sq2[t][:], sq[t][:])
+            nc.scalar.activation(sq[t], b_ps[t][:], ACT.Square)
+            nc.sync.dma_start(sq2[t][:], sq[t])
+
+        for t in range(PACK - 1):
+            leave_d(t)
+        square_b(0)
+        leave_d(PACK - 1)
+        for t in range(1, PACK):
+            square_b(t)
         for t in range(PACK):
             nc.scalar.activation(bg[t][:], b_ps[t][:], ACT.Copy, scale=gcol[:, 4 + t : 5 + t])
         y_ps = [bank(t) for t in range(PACK)]
         for t in range(PACK):
             product(2, t, y_ps[t])
-            nc.scalar.activation(yg[t][:], y_ps[t][:], ACT.Copy, scale=gcol[:, t : t + 1])
+            nc.scalar.activation(yg[t], y_ps[t][:], ACT.Copy, scale=gcol[:, t : t + 1])
 
         for t in range(PACK):
-            for lo in (0, HALF):
-                look_up(pr[t][:, lo : lo + HALF], dg[t], l2, lo, HALF, th[t][:, lo : lo + HALF], ALU.mult)
+            look_up(pr[t], dg_w[t], l2, 0, S, th[t], ALU.mult)
         for t in range(PACK):
-            for lo in (0, HALF):
-                look_up(us[t][:, lo : lo + HALF], sq[t], l3, lo, HALF, sq2[t][:, lo : lo + HALF], ALU.add)
-            nc.scalar.activation(rr[t][:], us[t][:], ACT.Abs_reciprocal_sqrt, bias=quarter[:])
+            look_up(us[t], sq_w[t], l3, 0, S, sq2[t][:], ALU.add)
+            nc.scalar.activation(rr[t][:], us[t], ACT.Abs_reciprocal_sqrt, bias=quarter[:])
         z = sb("z", [P, PACK, S], F32)
         for t in range(PACK):
-            for lo in (0, HALF):
-                look_up(z[:, t, lo : lo + HALF], yg[t], l1, lo, HALF, pr[t][:, lo : lo + HALF], ALU.subtract)
+            look_up(z[:, t, :], yg_w[t], l1, 0, S, pr[t], ALU.subtract)
         zb = sb("zb", [P, PACK * S], BF16)
         nc.scalar.copy(zb[:].rearrange("p (e m t) -> p m e t", e=4, t=4), z[:].rearrange("p t (m e) -> p m e t", e=4))
         zq = sb("zq", [P, S], U32)
         zs = sb("zs", [P, S], U8)
-
-        z2_parts = [(0, 256), (256, 128), (384, 128)]
         z2q = sb("z2q", [P, S], U32)
         z2s = sb("z2s", [P, S], U8)
         s_ps = [bank(4 + e) for e in range(PACK)]
         sw = planes("sw")
-        for k, (lo, n) in enumerate(z2_parts):
-            z2 = sb("z2_%d" % k, [P, PACK, n], F32)
-            z2b = sb("z2b_%d" % k, [P, PACK * n], BF16)
+
+        def weave(engine_copy, dst, src):
+            engine_copy(dst.rearrange("p (c i t) -> p c t i", i=4, t=4), src.rearrange("p t (c i) -> p c t i", i=4))
+
+        def z2_part(tag, lo, n):
+            z2 = keep.tile([P, PACK, n], F32, name="z2_%d" % lo, tag=tag, align_bytes=64)
             for t in range(PACK):
                 look_up(z2[:, t, :], bg[t], l4, lo, n, rr[t][:, lo : lo + n], ALU.mult)
-            if k == 0:
-                nc.vector.quantize_mx(out=zq[:].bitcast(FP8X4), scales=zs[:], in_=zb[:])
-            dst = z2b[:].rearrange("p (c i t) -> p c t i", i=4, t=4)
-            src = z2[:].rearrange("p t (c i) -> p c t i", i=4)
-            if k == len(z2_parts) - 1:
-                nc.vector.tensor_copy(dst, src)
-            else:
-                nc.scalar.copy(dst, src)
-            nc.vector.quantize_mx(out=z2q[:, lo : lo + n].bitcast(FP8X4), scales=z2s[:, lo : lo + n], in_=z2b[:])
+            return z2
+
+        def scores(lo, n):
             for e in range(PACK):
                 nc.tensor.matmul_mx(
                     out=s_ps[e][:, lo : lo + n],
@@ -182,14 +197,29 @@ def tile_picked_twksoftbrmstop2_none_po_kernel(tc, x_words, x_scales, w1_words, 
                 )
                 nc.scalar.activation(sw[e][:, lo : lo + n], s_ps[e][:, lo : lo + n], ACT.Copy, scale=0.03125)
 
+        z2_a = z2_part("z2_a", 0, HALF)
+        z2b_a = sb("z2b_a", [P, PACK * HALF], BF16)
+        weave(nc.scalar.copy, z2b_a[:], z2_a[:])
+        nc.vector.quantize_mx(out=zq[:].bitcast(FP8X4), scales=zs[:], in_=zb[:])
+        z2_b = z2_part("zb", HALF, P)
+        z2b_b = sb("z2b_b", [P, PACK * HALF], BF16)
+        weave(nc.scalar.copy, z2b_b[:, 0 : PACK * P], z2_b[:])
+        nc.vector.quantize_mx(out=z2q[:, 0:HALF].bitcast(FP8X4), scales=z2s[:, 0:HALF], in_=z2b_a[:])
+        scores(0, HALF)
+        z2_c = z2_part("z2b_a", HALF + P, P)
+        weave(nc.vector.tensor_copy, z2b_b[:, PACK * P :], z2_c[:])
+        nc.vector.quantize_mx(out=z2q[:, HALF:].bitcast(FP8X4), scales=z2s[:, HALF:], in_=z2b_b[:])
+        scores(HALF, HALF)
+
         oq = sb("oq", [P, S], I32)
         osc = sb("osc", [P, S], U8)
         out_rows = out_0.rearrange("(p e) v -> p e v", e=4)
         words_out = out_1[0].rearrange("p n t -> p (n t)").bitcast(I32)
-        parts = [(0, HALF), (HALF, HALF)]
+        parts = [(0, HALF), (HALF, P), (HALF + P, P)]
         st = []
         for k, (lo, n) in enumerate(parts):
-            st.append({nm: sb("%s_%d" % (nm, k), [P, PACK, n], F32) for nm in ("c", "u", "au", "hi", "pp", "tt", "o")})
+            st.append({nm: sb("%s_%d" % (nm, k), [P, PACK, n], F32) for nm in ("c", "hi", "tt", "o")})
+        ob = [sb("ob_0", [P, PACK * HALF], BF16), sb("ob_1", [P, PACK * HALF], BF16)]
 
         def pair(tile, a):
             return tile[:, 2 * a : 2 * a + 2, :].rearrange("p e v -> p (e v)")
@@ -198,60 +228,78 @@ def tile_picked_twksoftbrmstop2_none_po_kernel(tc, x_words, x_scales, w1_words, 
             lo, n = parts[k]
             look_up(st[k]["c"][:, e, :], sw[e], l7, lo, n, None, None)
 
-        def middle(k):
+        def middle(k, u_tag, au_tag, tag):
             lo, n = parts[k]
             s = st[k]
+            s["u"] = keep.tile([P, PACK, n], F32, name="u_%d" % k, tag=u_tag, align_bytes=64)
+            s["au"] = keep.tile([P, PACK, n], F32, name="au_%d" % k, tag=au_tag, align_bytes=64)
             for e in range(PACK):
                 look_up(s["u"][:, e, :], sw[e], l5, lo, n, s["c"][:, e, :], ALU.subtract)
                 if e % 2 == 1:
                     nc.scalar.activation(pair(s["au"], e // 2), pair(s["u"], e // 2), ACT.Abs)
             for a in range(2):
                 nc.vector.scalar_tensor_tensor(pair(s["hi"], a), pair(s["u"], a), 0.0, pair(s["c"], a), ALU.max, ALU.add)
+            s["pp"] = keep.tile([P, PACK, n], F32, name="pp_%d" % k, tag=tag, align_bytes=64)
             for e in range(PACK):
                 look_up(s["pp"][:, e, :], sw[e], l6, lo, n, s["hi"][:, e, :], ALU.subtract)
 
-        def last(k, step, a):
+        def summed(k, b):
+            lo, n = parts[k]
             s = st[k]
-            if step == 0:
-                nc.vector.scalar_tensor_tensor(pair(s["tt"], a), pair(s["pp"], a), -1.0, pair(s["au"], a), ALU.mult, ALU.min)
-            elif step == 1:
-                nc.vector.scalar_tensor_tensor(pair(s["u"], a), pair(s["tt"], a), -2.0, pair(s["tt"], a), ALU.mult, ALU.max)
-            else:
-                nc.vector.tensor_tensor(pair(s["o"], a), pair(s["u"], a), pair(s["hi"], a), ALU.add)
+            j = lo // P + b
+            cols = slice(P * b, P * b + P)
+            nc.vector.scalar_tensor_tensor(s["tt"][:, :, cols], s["pp"][:, :, cols], -1.0, s["au"][:, :, cols], ALU.mult, ALU.min)
+            neg = sb("neg_%d" % j, [P, PACK, P], F32)
+            nc.scalar.activation(neg[:], s["tt"][:, :, cols], ACT.Relu, scale=-3.0)
+            turned = bank(j)
+            for e in range(PACK):
+                terms = [s["hi"][:, e, cols], s["tt"][:, e, cols], neg[:, e, :]]
+                for i, term in enumerate(terms):
+                    nc.tensor.matmul(turned[:, P * e : P * e + P], term, ident[:], start=(i == 0), stop=(i == 2), is_transpose=True)
+            mid = sb("mid_%d" % j, [P, S], F32)
+            nc.scalar.copy(mid[:], turned[:])
+            back = bank(3 + j)
+            for e in range(PACK):
+                nc.tensor.transpose(back[:, P * e : P * e + P], mid[:, P * e : P * e + P], ident[:])
+            nc.scalar.copy(s["o"][:, :, cols], back[:].rearrange("p (e v) -> p e v", e=4))
+            half = ob[j // 2][:, PACK * P * (j % 2) : PACK * P * (j % 2 + 1)]
+            nc.scalar.copy(half.rearrange("p (v e) -> p v e", e=4), back[:].rearrange("p (e v) -> p v e", e=4))
 
-        def leave(k):
+        def store(k):
             lo, n = parts[k]
-            o = st[k]["o"]
-            nc.sync.dma_start(out_rows[:, :, lo : lo + n], o[:])
-            ob = sb("ob_%d" % k, [P, PACK * n], BF16)
-            dst = ob[:].rearrange("p (c i t) -> p c t i", i=4, t=4)
-            src = o[:].rearrange("p t (c i) -> p c t i", i=4)
-            if k == len(parts) - 1:
-                nc.vector.tensor_copy(dst, src)
-            else:
-                nc.scalar.copy(dst, src)
-            return ob
+            nc.sync.dma_start(out_rows[:, :, lo : lo + n], st[k]["o"][:])
 
-        def hand_on(k, ob):
-            lo, n = parts[k]
-            nc.vector.quantize_mx(out=oq[:, lo : lo + n].bitcast(U32).bitcast(FP8X4), scales=osc[:, lo : lo + n], in_=ob[:])
-            nc.scalar.dma_start(words_out[:, lo : lo + n], oq[:, lo : lo + n])
+        def hand_on(h):
+            cols = slice(HALF * h, HALF * h + HALF)
+            nc.vector.quantize_mx(out=oq[:, cols].bitcast(U32).bitcast(FP8X4), scales=osc[:, cols], in_=ob[h][:])
+            nc.scalar.dma_start(words_out[:, cols], oq[:, cols])
 
         for e in range(PACK):
             first(0, e)
-        middle(0)
-        for step in range(3):
-            for a in range(2):
-                last(0, step, a)
-            first(1, step)
-        first(1, 3)
-        ob0 = leave(0)
-        middle(1)
-        hand_on(0, ob0)
-        for step in range(3):
-            for a in range(2):
-                last(1, step, a)
-        hand_on(1, leave(1))
+        middle(0, "u_0", "au_0", "pp_0")
+        for e in range(PACK):
+            first(1, e)
+            if e < 2:
+                summed(0, e)
+        store(0)
+        middle(1, "u_1", "neg_0", "pp_1")
+        for e in range(PACK):
+            first(2, e)
+            if e == 0:
+                summed(1, 0)
+        store(1)
+        hand_on(0)
+        middle(2, "pp_1", "mid_1", "ob_0")
+        s = st[2]
+        for a in range(2):
+            nc.vector.scalar_tensor_tensor(pair(s["tt"], a), pair(s["pp"], a), -1.0, pair(s["au"], a), ALU.mult, ALU.min)
+        for a in range(2):
+            nc.vector.scalar_tensor_tensor(pair(s["u"], a), pair(s["tt"], a), -2.0, pair(s["tt"], a), ALU.mult, ALU.max)
+        for a in range(2):
+            nc.vector.tensor_tensor(pair(s["o"], a), pair(s["u"], a), pair(s["hi"], a), ALU.add)
+        store(2)
+        weave(nc.vector.tensor_copy, ob[1][:, PACK * P :], s["o"][:])
+        hand_on(1)
         for q in range(4):
             queue = nc.sync if q % 2 == 0 else nc.scalar
             queue.dma_start(out_2[0][4 * q : 4 * q + 4, :].bitcast(I32), osc[32 * q : 32 * q + 4, :].bitcast(I32))

@@ -41,35 +41,37 @@ def tile_picked_twksoftbrmstop2_none_po_kernel(tc, x_words, x_scales, w1_words, 
 
         def load_scale_rows(queue, dst, src):
             for q in range(4):
-                rows = src[0][4 * q : 4 * q + 4, :].bitcast(I32)
-                queue.dma_start(dst[32 * q : 32 * q + 32, :], rows.unsqueeze(0).broadcast_to([8, 4, rows.shape[1]]))
+                queue.dma_start(dst[32 * q : 32 * q + 4, :], src[0][4 * q : 4 * q + 4, :].bitcast(I32))
 
         xs = sb("xs", [P, T // 4], I32)
+        nc.gpsimd.memset(xs[:], 0)
         wsc = [sb("wsc%d" % i, [P, S // 4], I32) for i in range(3)]
         ww = [sb("ww%d" % i, [P, S // 2], I32) for i in range(3)]
         w_words = [w2_words, w3_words, w1_words]
         w_scales = [w2_scales, w3_scales, w1_scales]
         grow = sb("grow", [P, P], F32)
         nc.gpsimd.memset(grow[:], 0.0)
+        quarter = sb("quarter", [P, 1], F32)
+        nc.vector.memset(quarter[:], 0.25)
+        for i in range(3):
+            nc.vector.memset(wsc[i][:], 0)
         nc.gpsimd.dma_start(grow[0:4, :].rearrange("t (b r) -> t b r", r=8), ga.rearrange("(b t r) o -> t b (r o)", t=4, r=8))
         nc.gpsimd.dma_start(grow[4:8, :].rearrange("t (b r) -> t b r", r=8), gb.rearrange("(b t r) o -> t b (r o)", t=4, r=8))
         ident = sb("ident", [P, P], F32)
         make_identity(nc, ident[:])
-        quarter = sb("quarter", [P, 1], F32)
-        nc.gpsimd.memset(quarter[:], 0.25)
-        load_scale_rows(nc.gpsimd, wsc[2], w_scales[2])
 
         xw = sb("xw", [P, T], I32)
         l_two = load_list("l_two", two)
-        load_scale_rows(nc.sync, xs, x_scales)
-        nc.sync.dma_start(xw[:], x_words[0].rearrange("p n t -> p (n t)").bitcast(I32))
         l_three = load_list("l_three", three)
         l_offs = load_list("l_offs", offs)
-        load_scale_rows(nc.sync, wsc[0], w_scales[0])
-        nc.sync.dma_start(ww[0][:], w_words[0][0].bitcast(I32))
-        nc.sync.dma_start(ww[1][:], w_words[1][0].bitcast(I32))
-        load_scale_rows(nc.sync, wsc[1], w_scales[1])
-        l2 = load_list("l2", n2)
+        load_scale_rows(nc.sync, xs, x_scales)
+        nc.sync.dma_start(xw[:], x_words[0].rearrange("p n t -> p (n t)").bitcast(I32))
+        for i in range(2):
+            load_scale_rows(nc.sync, wsc[i], w_scales[i])
+            nc.sync.dma_start(ww[i][:], w_words[i][0].bitcast(I32))
+            if i == 0:
+                l2 = load_list("l2", n2)
+        load_scale_rows(nc.sync, wsc[2], w_scales[2])
         nc.sync.dma_start(ww[2][:], w_words[2][0].bitcast(I32))
         l3 = load_list("l3", n3)
         l1 = load_list("l1", n1)
@@ -85,7 +87,7 @@ def tile_picked_twksoftbrmstop2_none_po_kernel(tc, x_words, x_scales, w1_words, 
 
         lists = [l_two, l_three, l_offs]
         xs_g = [sb("xs_g%d" % i, [P, S], U8) for i in range(3)]
-        xw_tags = ["xw_g0", "wsc0", "xw_g2"]
+        xw_tags = ["xw_g0", "ww0", "wsc0"]
         xw_g = [keep.tile([P, S], U32, name="xw_g%d" % i, tag=xw_tags[i], align_bytes=64) for i in range(3)]
         wwd = [sb("wwd%d" % i, [P, S // 2], I32) for i in range(3)]
         wsd = [sb("wsd%d" % i, [P, S // 4], I32) for i in range(3)]
@@ -93,8 +95,8 @@ def tile_picked_twksoftbrmstop2_none_po_kernel(tc, x_words, x_scales, w1_words, 
             nc.vector.tensor_copy(xs_g[i][:], xs[:].bitcast(U8).indirect(lists[i][:]))
         for i in range(3):
             nc.vector.tensor_copy(xw_g[i][:], xw[:].bitcast(U32).indirect(lists[i][:]))
-            nc.vector.tensor_copy(wwd[i][:].rearrange("p (t b w) -> p t b w", t=4, w=4), ww[i][:].rearrange("p (b t w) -> p t b w", t=4, w=4))
             nc.vector.tensor_copy(wsd[i][:].rearrange("p (t b w) -> p t b w", t=4, w=2), wsc[i][:].rearrange("p (b t w) -> p t b w", t=4, w=2))
+            nc.vector.tensor_copy(wwd[i][:].rearrange("p (t b w) -> p t b w", t=4, w=4), ww[i][:].rearrange("p (b t w) -> p t b w", t=4, w=4))
 
         def product(i, t, acc):
             nc.tensor.matmul_mx(
@@ -121,14 +123,14 @@ def tile_picked_twksoftbrmstop2_none_po_kernel(tc, x_words, x_scales, w1_words, 
             return [keep.tile([P, 2 * S], F32, name="%s%d" % (name, t), tag=tags[t], align_bytes=64) for t in range(PACK)]
 
         dg_w = windows("dg", ["dg0", "dg1", "dg2", "dg3"])
-        sq_w = windows("sq", ["sq0", "wsc1", "sq2", "wsc2"])
+        sq_w = windows("sq", ["sq0", "ww1", "sq2", "ww2"])
         yg_w = windows("yg", ["yg0", "yg1", "yg2", "yg3"])
         dg = [w[:, 0:S] for w in dg_w]
         sq = [w[:, 0:S] for w in sq_w]
         yg = [w[:, 0:S] for w in yg_w]
         th_last = sb("th_last", [P, S], F32)
         th = [dg_w[t + 1][:, S:] for t in range(PACK - 1)] + [th_last[:]]
-        nc.gpsimd.memset(dg_w[0][:, S:], 0.0)
+        nc.vector.memset(dg_w[0][:, S:], 0.0)
         us = [w[:, S:] for w in yg_w]
         sq2, bg = planes("sqc"), planes("bg")
         rr = planes("rr")
@@ -143,20 +145,18 @@ def tile_picked_twksoftbrmstop2_none_po_kernel(tc, x_words, x_scales, w1_words, 
         def square_b(t):
             product(1, t, b_ps[t])
             nc.scalar.activation(sq[t], b_ps[t][:], ACT.Square)
-            nc.sync.dma_start(sq2[t][:], sq[t])
+            nc.scalar.activation(sq2[t][:], b_ps[t][:], ACT.Square)
 
-        for t in range(PACK - 1):
-            leave_d(t)
-        square_b(0)
-        leave_d(PACK - 1)
-        for t in range(1, PACK):
-            square_b(t)
         for t in range(PACK):
-            nc.scalar.activation(bg[t][:], b_ps[t][:], ACT.Copy, scale=gcol[:, 4 + t : 5 + t])
+            leave_d(t)
+        for t in range(PACK):
+            square_b(t)
         y_ps = [bank(t) for t in range(PACK)]
         for t in range(PACK):
             product(2, t, y_ps[t])
             nc.scalar.activation(yg[t], y_ps[t][:], ACT.Copy, scale=gcol[:, t : t + 1])
+        for t in range(PACK):
+            nc.scalar.activation(bg[t][:], b_ps[t][:], ACT.Copy, scale=gcol[:, 4 + t : 5 + t])
 
         for t in range(PACK):
             look_up(pr[t], dg_w[t], l2, 0, S, th[t], ALU.mult)
@@ -208,17 +208,20 @@ def tile_picked_twksoftbrmstop2_none_po_kernel(tc, x_words, x_scales, w1_words, 
         scores(0, HALF)
         z2_c = z2_part("z2b_a", HALF + P, P)
         weave(nc.vector.tensor_copy, z2b_b[:, PACK * P :], z2_c[:])
-        nc.vector.quantize_mx(out=z2q[:, HALF:].bitcast(FP8X4), scales=z2s[:, HALF:], in_=z2b_b[:])
+        for b in range(2):
+            cols = slice(HALF + P * b, HALF + P * b + P)
+            nc.vector.quantize_mx(out=z2q[:, cols].bitcast(FP8X4), scales=z2s[:, cols], in_=z2b_b[:, PACK * P * b : PACK * P * (b + 1)])
         scores(HALF, HALF)
 
         oq = sb("oq", [P, S], I32)
         osc = sb("osc", [P, S], U8)
         out_rows = out_0.rearrange("(p e) v -> p e v", e=4)
         words_out = out_1[0].rearrange("p n t -> p (n t)").bitcast(I32)
-        parts = [(0, HALF), (HALF, P), (HALF + P, P)]
+        parts = [(0, HALF), (HALF, HALF)]
         st = []
         for k, (lo, n) in enumerate(parts):
-            st.append({nm: sb("%s_%d" % (nm, k), [P, PACK, n], F32) for nm in ("c", "hi", "tt", "o")})
+            st.append({nm: sb("%s_%d" % (nm, k), [P, PACK, n], F32) for nm in ("c", "hi", "tt")})
+        st[0]["o"] = sb("o_0", [P, PACK, HALF], F32)
         ob = [sb("ob_0", [P, PACK * HALF], BF16), sb("ob_1", [P, PACK * HALF], BF16)]
 
         def pair(tile, a):
@@ -282,23 +285,19 @@ def tile_picked_twksoftbrmstop2_none_po_kernel(tc, x_words, x_scales, w1_words, 
             if e < 2:
                 summed(0, e)
         store(0)
-        middle(1, "u_1", "neg_0", "pp_1")
-        for e in range(PACK):
-            first(2, e)
-            if e == 0:
-                summed(1, 0)
-        store(1)
         hand_on(0)
-        middle(2, "pp_1", "mid_1", "ob_0")
-        s = st[2]
-        for a in range(2):
-            nc.vector.scalar_tensor_tensor(pair(s["tt"], a), pair(s["pp"], a), -1.0, pair(s["au"], a), ALU.mult, ALU.min)
-        for a in range(2):
-            nc.vector.scalar_tensor_tensor(pair(s["u"], a), pair(s["tt"], a), -2.0, pair(s["tt"], a), ALU.mult, ALU.max)
-        for a in range(2):
-            nc.vector.tensor_tensor(pair(s["o"], a), pair(s["u"], a), pair(s["hi"], a), ALU.add)
-        store(2)
-        weave(nc.vector.tensor_copy, ob[1][:, PACK * P :], s["o"][:])
+        middle(1, "u_1", "neg_0", "pp_1")
+        s = st[1]
+        blocks = [slice(0, P), slice(P, HALF)]
+        for cols in blocks:
+            nc.vector.scalar_tensor_tensor(s["tt"][:, :, cols], s["pp"][:, :, cols], -1.0, s["au"][:, :, cols], ALU.mult, ALU.min)
+        for cols in blocks:
+            nc.vector.scalar_tensor_tensor(s["u"][:, :, cols], s["tt"][:, :, cols], -2.0, s["tt"][:, :, cols], ALU.mult, ALU.max)
+        for b, cols in enumerate(blocks):
+            o = keep.tile([P, PACK, P], F32, name="o_1%d" % b, tag=["o_10", "ob_0"][b], align_bytes=64)
+            nc.vector.tensor_tensor(o[:], s["u"][:, :, cols], s["hi"][:, :, cols], ALU.add)
+            nc.sync.dma_start(out_rows[:, :, HALF + P * b : HALF + P * b + P], o[:])
+            weave([nc.scalar.copy, nc.vector.tensor_copy][b], ob[1][:, PACK * P * b : PACK * P * (b + 1)], o[:])
         hand_on(1)
         for q in range(4):
             queue = nc.sync if q % 2 == 0 else nc.scalar

@@ -15,290 +15,312 @@ ALU = mybir.AluOpType
 ACT = mybir.ActivationFunctionType
 
 P = 128
-T = 2048
+TOKENS = 2048
 S = 512
 PACK = 4
-HALF = 256
+HALF = S // 2
+RUN = 8
+LIST_ROWS = 16
+HALF_SCORE_SCALE = 0.0625 / 2
 FLOPS = 4 * 2 * 512 * 512 * 512
 
 
-def tile_picked_twksoftbrmstop2_none_po_kernel(tc, x_words, x_scales, w1_words, w1_scales, w2_words, w2_scales, w3_words, w3_scales, ga, gb, offs, two, n1, n2, three, n3, n4, n5, n6, n7, out_0, out_1, out_2):
+def tile_picked_twksoftbrmstop2_none_po_kernel(
+    tc, x_words, x_scales, w1_words, w1_scales, w2_words, w2_scales, w3_words, w3_scales, ga, gb,
+    offs, two, n1, n2, three, n3, n4, n5, n6, n7, out_0, out_1, out_2,
+):
     nc = tc.nc
     with ExitStack() as ctx:
         keep = ctx.enter_context(tc.tile_pool(name="keep", bufs=1))
         psum = ctx.enter_context(tc.psum_pool(name="psum", bufs=1))
 
-        def sb(name, shape, dtype):
-            return keep.tile(shape, dtype, name=name, align_bytes=64)
+        def sbuf(name, shape, dtype, over=None):
+            return keep.tile(shape, dtype, name=name, tag=over or name, align_bytes=64)
 
-        def bank(k):
-            return psum.tile([P, S], F32, name="bank%d" % k, tag="bank%d" % k)
+        def bank(number):
+            return psum.tile([P, S], F32, name="bank%d" % number, tag="bank%d" % number)
+
+        def planes(name, width=S, over=(None,) * PACK):
+            return [sbuf("%s%d" % (name, t), [P, width], F32, over[t]) for t in range(PACK)]
 
         def load_list(name, src):
-            tile = keep.tile([P, S // 16], U16, name=name)
+            tile = keep.tile([P, S // LIST_ROWS], U16, name=name)
             nc.sync.dma_start(tile[:], src)
             return tile
 
-        def load_scale_rows(queue, dst, src):
+        def load_scale_rows(dst, src):
             for q in range(4):
-                queue.dma_start(dst[32 * q : 32 * q + 4, :], src[0][4 * q : 4 * q + 4, :].bitcast(I32))
+                nc.sync.dma_start(dst[32 * q : 32 * q + 4, :], src[0][4 * q : 4 * q + 4, :].bitcast(I32))
 
-        xs = sb("xs", [P, T // 4], I32)
-        nc.gpsimd.memset(xs[:], 0)
-        wsc = [sb("wsc%d" % i, [P, S // 4], I32) for i in range(3)]
-        ww = [sb("ww%d" % i, [P, S // 2], I32) for i in range(3)]
-        w_words = [w2_words, w3_words, w1_words]
-        w_scales = [w2_scales, w3_scales, w1_scales]
-        grow = sb("grow", [P, P], F32)
-        nc.gpsimd.memset(grow[:], 0.0)
-        quarter = sb("quarter", [P, 1], F32)
-        nc.vector.memset(quarter[:], 0.25)
-        for i in range(3):
-            nc.vector.memset(wsc[i][:], 0)
-        nc.gpsimd.dma_start(grow[0:4, :].rearrange("t (b r) -> t b r", r=8), ga.rearrange("(b t r) o -> t b (r o)", t=4, r=8))
-        nc.gpsimd.dma_start(grow[4:8, :].rearrange("t (b r) -> t b r", r=8), gb.rearrange("(b t r) o -> t b (r o)", t=4, r=8))
-        ident = sb("ident", [P, P], F32)
-        make_identity(nc, ident[:])
-
-        xw = sb("xw", [P, T], I32)
-        l_two = load_list("l_two", two)
-        l_three = load_list("l_three", three)
-        l_offs = load_list("l_offs", offs)
-        load_scale_rows(nc.sync, xs, x_scales)
-        nc.sync.dma_start(xw[:], x_words[0].rearrange("p n t -> p (n t)").bitcast(I32))
-        for i in range(2):
-            load_scale_rows(nc.sync, wsc[i], w_scales[i])
-            nc.sync.dma_start(ww[i][:], w_words[i][0].bitcast(I32))
-            if i == 0:
-                l2 = load_list("l2", n2)
-        load_scale_rows(nc.sync, wsc[2], w_scales[2])
-        nc.sync.dma_start(ww[2][:], w_words[2][0].bitcast(I32))
-        l3 = load_list("l3", n3)
-        l1 = load_list("l1", n1)
-        l4 = load_list("l4", n4)
-        l7 = load_list("l7", n7)
-        l5 = load_list("l5", n5)
-        l6 = load_list("l6", n6)
-
-        gps = bank(7)
-        nc.tensor.transpose(gps[:, 0:P], grow[:], ident[:])
-        gcol = sb("gcol", [P, 8], F32)
-        nc.scalar.copy(gcol[:], gps[:, 0:8])
-
-        lists = [l_two, l_three, l_offs]
-        xs_g = [sb("xs_g%d" % i, [P, S], U8) for i in range(3)]
-        xw_tags = ["xw_g0", "ww0", "wsc0"]
-        xw_g = [keep.tile([P, S], U32, name="xw_g%d" % i, tag=xw_tags[i], align_bytes=64) for i in range(3)]
-        wwd = [sb("wwd%d" % i, [P, S // 2], I32) for i in range(3)]
-        wsd = [sb("wsd%d" % i, [P, S // 4], I32) for i in range(3)]
-        for i in range(3):
-            nc.vector.tensor_copy(xs_g[i][:], xs[:].bitcast(U8).indirect(lists[i][:]))
-        for i in range(3):
-            nc.vector.tensor_copy(xw_g[i][:], xw[:].bitcast(U32).indirect(lists[i][:]))
-            nc.vector.tensor_copy(wsd[i][:].rearrange("p (t b w) -> p t b w", t=4, w=2), wsc[i][:].rearrange("p (b t w) -> p t b w", t=4, w=2))
-            nc.vector.tensor_copy(wwd[i][:].rearrange("p (t b w) -> p t b w", t=4, w=4), ww[i][:].rearrange("p (b t w) -> p t b w", t=4, w=4))
-
-        def product(i, t, acc):
-            nc.tensor.matmul_mx(
-                out=acc[:],
-                lhsT=wwd[i][:, 64 * t : 64 * t + 64].bitcast(U8).bitcast(FP4X4),
-                lhsT_scale=wsd[i][:, 32 * t : 32 * t + 32].bitcast(U8),
-                rhs=xw_g[i][:].bitcast(FP8X4),
-                rhs_scale=xs_g[i][:],
-                start=True,
-                stop=True,
-            )
-
-        def planes(name):
-            return [sb("%s%d" % (name, t), [P, S], F32) for t in range(PACK)]
-
-        def look_up(out, window, lst, lo, n, other, op):
-            picked = window[:].indirect(lst[:, lo // 16 : (lo + n) // 16])
+        def look_up(out, window, offsets, lo, n, other=None, op=None):
+            picked = window[:].indirect(offsets[:, lo // LIST_ROWS : (lo + n) // LIST_ROWS])
             if other is None:
                 nc.vector.tensor_copy(out, picked)
             else:
                 nc.vector.tensor_tensor(out, picked, other, op)
 
-        def windows(name, tags):
-            return [keep.tile([P, 2 * S], F32, name="%s%d" % (name, t), tag=tags[t], align_bytes=64) for t in range(PACK)]
+        def weave(copy, dst, src):
+            copy(dst.rearrange("p (c i t) -> p c t i", i=4, t=PACK), src.rearrange("p t (c i) -> p c t i", i=4))
 
-        dg_w = windows("dg", ["dg0", "dg1", "dg2", "dg3"])
-        sq_w = windows("sq", ["sq0", "ww1", "sq2", "ww2"])
-        yg_w = windows("yg", ["yg0", "yg1", "yg2", "yg3"])
-        dg = [w[:, 0:S] for w in dg_w]
-        sq = [w[:, 0:S] for w in sq_w]
-        yg = [w[:, 0:S] for w in yg_w]
-        th_last = sb("th_last", [P, S], F32)
-        th = [dg_w[t + 1][:, S:] for t in range(PACK - 1)] + [th_last[:]]
-        nc.vector.memset(dg_w[0][:, S:], 0.0)
-        us = [w[:, S:] for w in yg_w]
-        sq2, bg = planes("sqc"), planes("bg")
-        rr = planes("rr")
-        pr = [w[:, S:] for w in sq_w]
-        d_ps = [bank(t) for t in range(PACK)]
-        b_ps = [bank(4 + t) for t in range(PACK)]
-        def leave_d(t):
-            product(0, t, d_ps[t])
-            nc.scalar.activation(th[t], d_ps[t][:], ACT.Tanh)
-            nc.scalar.activation(dg[t], d_ps[t][:], ACT.Copy, scale=gcol[:, t : t + 1])
+        x_scale = sbuf("x_scale", [P, TOKENS // 4], I32)
+        nc.gpsimd.memset(x_scale[:], 0)
+        w_scale = [sbuf("w_scale%d" % i, [P, S // 4], I32) for i in range(3)]
+        w_code = [sbuf("w_code%d" % i, [P, S // 2], I32) for i in range(3)]
+        w_words = [w2_words, w3_words, w1_words]
+        w_scales = [w2_scales, w3_scales, w1_scales]
+        gain_rows = sbuf("gain_rows", [P, P], F32)
+        nc.gpsimd.memset(gain_rows[:], 0.0)
+        quarter = sbuf("quarter", [P, 1], F32)
+        nc.vector.memset(quarter[:], 0.25)
+        for i in range(3):
+            nc.vector.memset(w_scale[i][:], 0)
+        for first_row, gain in ((0, ga), (PACK, gb)):
+            nc.gpsimd.dma_start(
+                gain_rows[first_row : first_row + PACK, :].rearrange("t (b r) -> t b r", r=RUN),
+                gain.rearrange("(b t r) o -> t b (r o)", t=PACK, r=RUN),
+            )
+        ident = sbuf("ident", [P, P], F32)
+        make_identity(nc, ident[:])
 
-        def square_b(t):
-            product(1, t, b_ps[t])
-            nc.scalar.activation(sq[t], b_ps[t][:], ACT.Square)
-            nc.scalar.activation(sq2[t][:], b_ps[t][:], ACT.Square)
+        x_code = sbuf("x_code", [P, TOKENS], I32)
+        token_lists = [load_list("two", two), load_list("three", three), load_list("offs", offs)]
+        load_scale_rows(x_scale, x_scales)
+        nc.sync.dma_start(x_code[:], x_words[0].rearrange("p n t -> p (n t)").bitcast(I32))
+
+        def load_weight(i):
+            load_scale_rows(w_scale[i], w_scales[i])
+            nc.sync.dma_start(w_code[i][:], w_words[i][0].bitcast(I32))
+
+        load_weight(0)
+        list2 = load_list("list2", n2)
+        load_weight(1)
+        load_weight(2)
+        list3 = load_list("list3", n3)
+        list1 = load_list("list1", n1)
+        list4 = load_list("list4", n4)
+        list7 = load_list("list7", n7)
+        list5 = load_list("list5", n5)
+        list6 = load_list("list6", n6)
+
+        gain_bank = bank(7)
+        nc.tensor.transpose(gain_bank[:, 0:P], gain_rows[:], ident[:])
+        gain_cols = sbuf("gain_cols", [P, 2 * PACK], F32)
+        nc.scalar.copy(gain_cols[:], gain_bank[:, 0 : 2 * PACK])
+
+        picked_scale = [sbuf("picked_scale%d" % i, [P, S], U8) for i in range(3)]
+        staging_taken = [None, "w_code0", "w_scale0"]
+        picked_code = [sbuf("picked_code%d" % i, [P, S], U32, staging_taken[i]) for i in range(3)]
+        dealt_code = [sbuf("dealt_code%d" % i, [P, S // 2], I32) for i in range(3)]
+        dealt_scale = [sbuf("dealt_scale%d" % i, [P, S // 4], I32) for i in range(3)]
+
+        def deal(dst, src, run_words):
+            nc.vector.tensor_copy(
+                dst[:].rearrange("p (t b w) -> p t b w", t=PACK, w=run_words),
+                src[:].rearrange("p (b t w) -> p t b w", t=PACK, w=run_words),
+            )
+
+        for i in range(3):
+            nc.vector.tensor_copy(picked_scale[i][:], x_scale[:].bitcast(U8).indirect(token_lists[i][:]))
+        for i in range(3):
+            nc.vector.tensor_copy(picked_code[i][:], x_code[:].bitcast(U32).indirect(token_lists[i][:]))
+            deal(dealt_scale[i], w_scale[i], RUN // 4)
+            deal(dealt_code[i], w_code[i], RUN // 2)
+
+        def product(i, t, acc):
+            code_words, scale_words = P // 2, P // 4
+            nc.tensor.matmul_mx(
+                out=acc[:],
+                lhsT=dealt_code[i][:, code_words * t : code_words * (t + 1)].bitcast(U8).bitcast(FP4X4),
+                lhsT_scale=dealt_scale[i][:, scale_words * t : scale_words * (t + 1)].bitcast(U8),
+                rhs=picked_code[i][:].bitcast(FP8X4),
+                rhs_scale=picked_scale[i][:],
+                start=True,
+                stop=True,
+            )
+
+        d_win = planes("d_win", 2 * S)
+        sq_win = planes("sq_win", 2 * S, (None, "w_code1", None, "w_code2"))
+        y_win = planes("y_win", 2 * S)
+        tanh_last = sbuf("tanh_last", [P, S], F32)
+        tanh_d = [d_win[t + 1][:, S:] for t in range(PACK - 1)] + [tanh_last[:]]
+        nc.vector.memset(d_win[0][:, S:], 0.0)
+        under_root = [w[:, S:] for w in y_win]
+        b_win, sq_plain = planes("b_win"), planes("sq_plain")
+        s_win = planes("s_win", 2 * S)
+        inv_root = [w[:, S:] for w in s_win]
+        d_term = [w[:, S:] for w in sq_win]
+
+        d_banks = [bank(t) for t in range(PACK)]
+        b_banks = [bank(PACK + t) for t in range(PACK)]
+        for t in range(PACK):
+            product(0, t, d_banks[t])
+            nc.scalar.activation(tanh_d[t], d_banks[t][:], ACT.Tanh)
+            nc.scalar.activation(d_win[t][:, 0:S], d_banks[t][:], ACT.Copy, scale=gain_cols[:, t : t + 1])
+        for t in range(PACK):
+            product(1, t, b_banks[t])
+            nc.scalar.activation(sq_win[t][:, 0:S], b_banks[t][:], ACT.Square)
+            nc.scalar.activation(sq_plain[t][:], b_banks[t][:], ACT.Square)
+        y_banks = [bank(t) for t in range(PACK)]
+        for t in range(PACK):
+            product(2, t, y_banks[t])
+            nc.scalar.activation(y_win[t][:, 0:S], y_banks[t][:], ACT.Copy, scale=gain_cols[:, t : t + 1])
+        for t in range(PACK):
+            nc.scalar.activation(b_win[t][:], b_banks[t][:], ACT.Copy, scale=gain_cols[:, PACK + t : PACK + t + 1])
 
         for t in range(PACK):
-            leave_d(t)
+            look_up(d_term[t], d_win[t], list2, 0, S, tanh_d[t], ALU.mult)
         for t in range(PACK):
-            square_b(t)
-        y_ps = [bank(t) for t in range(PACK)]
+            look_up(under_root[t], sq_win[t], list3, 0, S, sq_plain[t][:], ALU.add)
+            nc.scalar.activation(inv_root[t], under_root[t], ACT.Abs_reciprocal_sqrt, bias=quarter[:])
+        z = sbuf("z", [P, PACK, S], F32)
         for t in range(PACK):
-            product(2, t, y_ps[t])
-            nc.scalar.activation(yg[t], y_ps[t][:], ACT.Copy, scale=gcol[:, t : t + 1])
-        for t in range(PACK):
-            nc.scalar.activation(bg[t][:], b_ps[t][:], ACT.Copy, scale=gcol[:, 4 + t : 5 + t])
+            look_up(z[:, t, :], y_win[t], list1, 0, S, d_term[t], ALU.subtract)
+        z_woven = sbuf("z_woven", [P, PACK * S], BF16)
+        nc.scalar.copy(
+            z_woven[:].rearrange("p (e m t) -> p m e t", e=PACK, t=PACK),
+            z[:].rearrange("p t (m e) -> p m e t", e=PACK),
+        )
+        z_code = sbuf("z_code", [P, S], U32)
+        z_scale = sbuf("z_scale", [P, S], U8)
+        z2_code = sbuf("z2_code", [P, S], U32)
+        z2_scale = sbuf("z2_scale", [P, S], U8)
+        s_banks = [bank(PACK + e) for e in range(PACK)]
 
-        for t in range(PACK):
-            look_up(pr[t], dg_w[t], l2, 0, S, th[t], ALU.mult)
-        for t in range(PACK):
-            look_up(us[t], sq_w[t], l3, 0, S, sq2[t][:], ALU.add)
-            nc.scalar.activation(rr[t][:], us[t], ACT.Abs_reciprocal_sqrt, bias=quarter[:])
-        z = sb("z", [P, PACK, S], F32)
-        for t in range(PACK):
-            look_up(z[:, t, :], yg_w[t], l1, 0, S, pr[t], ALU.subtract)
-        zb = sb("zb", [P, PACK * S], BF16)
-        nc.scalar.copy(zb[:].rearrange("p (e m t) -> p m e t", e=4, t=4), z[:].rearrange("p t (m e) -> p m e t", e=4))
-        zq = sb("zq", [P, S], U32)
-        zs = sb("zs", [P, S], U8)
-        z2q = sb("z2q", [P, S], U32)
-        z2s = sb("z2s", [P, S], U8)
-        s_ps = [bank(4 + e) for e in range(PACK)]
-        sw = planes("sw")
-
-        def weave(engine_copy, dst, src):
-            engine_copy(dst.rearrange("p (c i t) -> p c t i", i=4, t=4), src.rearrange("p t (c i) -> p c t i", i=4))
-
-        def z2_part(tag, lo, n):
-            z2 = keep.tile([P, PACK, n], F32, name="z2_%d" % lo, tag=tag, align_bytes=64)
+        def z2_columns(lo, n, over):
+            z2 = sbuf("z2_from%d" % lo, [P, PACK, n], F32, over)
             for t in range(PACK):
-                look_up(z2[:, t, :], bg[t], l4, lo, n, rr[t][:, lo : lo + n], ALU.mult)
+                look_up(z2[:, t, :], b_win[t], list4, lo, n, inv_root[t][:, lo : lo + n], ALU.mult)
             return z2
+
+        def quantise(code, scale, lo, n, woven):
+            nc.vector.quantize_mx(out=code[:, lo : lo + n].bitcast(FP8X4), scales=scale[:, lo : lo + n], in_=woven)
 
         def scores(lo, n):
             for e in range(PACK):
                 nc.tensor.matmul_mx(
-                    out=s_ps[e][:, lo : lo + n],
-                    lhsT=zq[:, P * e : P * e + P].bitcast(FP8X4),
-                    lhsT_scale=zs[:, P * e : P * e + P],
-                    rhs=z2q[:, lo : lo + n].bitcast(FP8X4),
-                    rhs_scale=z2s[:, lo : lo + n],
+                    out=s_banks[e][:, lo : lo + n],
+                    lhsT=z_code[:, P * e : P * e + P].bitcast(FP8X4),
+                    lhsT_scale=z_scale[:, P * e : P * e + P],
+                    rhs=z2_code[:, lo : lo + n].bitcast(FP8X4),
+                    rhs_scale=z2_scale[:, lo : lo + n],
                     start=True,
                     stop=True,
                 )
-                nc.scalar.activation(sw[e][:, lo : lo + n], s_ps[e][:, lo : lo + n], ACT.Copy, scale=0.03125)
+                nc.scalar.activation(s_win[e][:, lo : lo + n], s_banks[e][:, lo : lo + n], ACT.Copy, scale=HALF_SCORE_SCALE)
 
-        z2_a = z2_part("z2_a", 0, HALF)
-        z2b_a = sb("z2b_a", [P, PACK * HALF], BF16)
-        weave(nc.scalar.copy, z2b_a[:], z2_a[:])
-        nc.vector.quantize_mx(out=zq[:].bitcast(FP8X4), scales=zs[:], in_=zb[:])
-        z2_b = z2_part("zb", HALF, P)
-        z2b_b = sb("z2b_b", [P, PACK * HALF], BF16)
-        weave(nc.scalar.copy, z2b_b[:, 0 : PACK * P], z2_b[:])
-        nc.vector.quantize_mx(out=z2q[:, 0:HALF].bitcast(FP8X4), scales=z2s[:, 0:HALF], in_=z2b_a[:])
+        z2_first = z2_columns(0, HALF, None)
+        z2_woven_first = sbuf("z2_woven_first", [P, PACK * HALF], BF16)
+        weave(nc.scalar.copy, z2_woven_first[:], z2_first[:])
+        quantise(z_code, z_scale, 0, S, z_woven[:])
+        z2_third_quarter = z2_columns(HALF, P, "z_woven")
+        z2_woven_second = sbuf("z2_woven_second", [P, PACK * HALF], BF16)
+        weave(nc.scalar.copy, z2_woven_second[:, 0 : PACK * P], z2_third_quarter[:])
+        quantise(z2_code, z2_scale, 0, HALF, z2_woven_first[:])
         scores(0, HALF)
-        z2_c = z2_part("z2b_a", HALF + P, P)
-        weave(nc.vector.tensor_copy, z2b_b[:, PACK * P :], z2_c[:])
-        for b in range(2):
-            cols = slice(HALF + P * b, HALF + P * b + P)
-            nc.vector.quantize_mx(out=z2q[:, cols].bitcast(FP8X4), scales=z2s[:, cols], in_=z2b_b[:, PACK * P * b : PACK * P * (b + 1)])
+        z2_last_quarter = z2_columns(HALF + P, P, "z2_woven_first")
+        weave(nc.vector.tensor_copy, z2_woven_second[:, PACK * P :], z2_last_quarter[:])
+        for blk in range(2):
+            quantise(z2_code, z2_scale, HALF + P * blk, P, z2_woven_second[:, PACK * P * blk : PACK * P * (blk + 1)])
         scores(HALF, HALF)
 
-        oq = sb("oq", [P, S], I32)
-        osc = sb("osc", [P, S], U8)
-        out_rows = out_0.rearrange("(p e) v -> p e v", e=4)
-        words_out = out_1[0].rearrange("p n t -> p (n t)").bitcast(I32)
-        parts = [(0, HALF), (HALF, HALF)]
-        st = []
-        for k, (lo, n) in enumerate(parts):
-            st.append({nm: sb("%s_%d" % (nm, k), [P, PACK, n], F32) for nm in ("c", "hi", "tt")})
-        st[0]["o"] = sb("o_0", [P, PACK, HALF], F32)
-        ob = [sb("ob_0", [P, PACK * HALF], BF16), sb("ob_1", [P, PACK * HALF], BF16)]
-
-        def pair(tile, a):
-            return tile[:, 2 * a : 2 * a + 2, :].rearrange("p e v -> p (e v)")
-
-        def first(k, e):
-            lo, n = parts[k]
-            look_up(st[k]["c"][:, e, :], sw[e], l7, lo, n, None, None)
-
-        def middle(k, u_tag, au_tag, tag):
-            lo, n = parts[k]
-            s = st[k]
-            s["u"] = keep.tile([P, PACK, n], F32, name="u_%d" % k, tag=u_tag, align_bytes=64)
-            s["au"] = keep.tile([P, PACK, n], F32, name="au_%d" % k, tag=au_tag, align_bytes=64)
-            for e in range(PACK):
-                look_up(s["u"][:, e, :], sw[e], l5, lo, n, s["c"][:, e, :], ALU.subtract)
-                if e % 2 == 1:
-                    nc.scalar.activation(pair(s["au"], e // 2), pair(s["u"], e // 2), ACT.Abs)
-            for a in range(2):
-                nc.vector.scalar_tensor_tensor(pair(s["hi"], a), pair(s["u"], a), 0.0, pair(s["c"], a), ALU.max, ALU.add)
-            s["pp"] = keep.tile([P, PACK, n], F32, name="pp_%d" % k, tag=tag, align_bytes=64)
-            for e in range(PACK):
-                look_up(s["pp"][:, e, :], sw[e], l6, lo, n, s["hi"][:, e, :], ALU.subtract)
-
-        def summed(k, b):
-            lo, n = parts[k]
-            s = st[k]
-            j = lo // P + b
-            cols = slice(P * b, P * b + P)
-            nc.vector.scalar_tensor_tensor(s["tt"][:, :, cols], s["pp"][:, :, cols], -1.0, s["au"][:, :, cols], ALU.mult, ALU.min)
-            neg = sb("neg_%d" % j, [P, PACK, P], F32)
-            nc.scalar.activation(neg[:], s["tt"][:, :, cols], ACT.Relu, scale=-3.0)
-            turned = bank(j)
-            for e in range(PACK):
-                terms = [s["hi"][:, e, cols], s["tt"][:, e, cols], neg[:, e, :]]
-                for i, term in enumerate(terms):
-                    nc.tensor.matmul(turned[:, P * e : P * e + P], term, ident[:], start=(i == 0), stop=(i == 2), is_transpose=True)
-            mid = sb("mid_%d" % j, [P, S], F32)
-            nc.scalar.copy(mid[:], turned[:])
-            back = bank(3 + j)
-            for e in range(PACK):
-                nc.tensor.transpose(back[:, P * e : P * e + P], mid[:, P * e : P * e + P], ident[:])
-            nc.scalar.copy(s["o"][:, :, cols], back[:].rearrange("p (e v) -> p e v", e=4))
-            half = ob[j // 2][:, PACK * P * (j % 2) : PACK * P * (j % 2 + 1)]
-            nc.scalar.copy(half.rearrange("p (v e) -> p v e", e=4), back[:].rearrange("p (e v) -> p v e", e=4))
-
-        def store(k):
-            lo, n = parts[k]
-            nc.sync.dma_start(out_rows[:, :, lo : lo + n], st[k]["o"][:])
-
-        def hand_on(h):
-            cols = slice(HALF * h, HALF * h + HALF)
-            nc.vector.quantize_mx(out=oq[:, cols].bitcast(U32).bitcast(FP8X4), scales=osc[:, cols], in_=ob[h][:])
-            nc.scalar.dma_start(words_out[:, cols], oq[:, cols])
-
-        for e in range(PACK):
-            first(0, e)
-        middle(0, "u_0", "au_0", "pp_0")
-        for e in range(PACK):
-            first(1, e)
-            if e < 2:
-                summed(0, e)
-        store(0)
-        hand_on(0)
-        middle(1, "u_1", "neg_0", "pp_1")
-        s = st[1]
+        out_code = sbuf("out_code", [P, S], I32)
+        out_scale = sbuf("out_scale", [P, S], U8)
+        out_rows = out_0.rearrange("(p e) v -> p e v", e=PACK)
+        out_words = out_1[0].rearrange("p n t -> p (n t)").bitcast(I32)
         blocks = [slice(0, P), slice(P, HALF)]
+
+        def half_tiles(name, h, over=None):
+            return sbuf("%s%d" % (name, h), [P, PACK, HALF], F32, over)
+
+        hi, low = zip(*[(half_tiles("hi", h), half_tiles("low", h)) for h in range(2)])
+        out_first = half_tiles("out_half", 0)
+        out_woven = [sbuf("out_woven%d" % h, [P, PACK * HALF], BF16) for h in range(2)]
+        c = sbuf("c", [P, PACK, S], F32)
+
+        def a_less_c(h, e, diff):
+            look_up(diff[:, e, :], s_win[e], list5, HALF * h, HALF, c[:, e, HALF * h : HALF * (h + 1)], ALU.subtract)
+
+        def gap_and_hi(h, diff, over):
+            gap = half_tiles("gap", h, over)
+            for first in (0, 2):
+                two_planes = slice(first, first + 2)
+                nc.scalar.activation(
+                    gap[:, two_planes, :].rearrange("p e v -> p (e v)"),
+                    diff[:, two_planes, :].rearrange("p e v -> p (e v)"),
+                    ACT.Abs,
+                )
+                nc.vector.scalar_tensor_tensor(
+                    hi[h][:, two_planes, :], diff[:, two_planes, :], 0.0,
+                    c[:, two_planes, HALF * h : HALF * (h + 1)], ALU.max, ALU.add,
+                )
+            return gap
+
+        def b_less_hi(h):
+            above = half_tiles("above", h)
+            for e in range(PACK):
+                look_up(above[:, e, :], s_win[e], list6, HALF * h, HALF, hi[h][:, e, :], ALU.subtract)
+            return above
+
+        def lower(h, cols, above, gap):
+            nc.vector.scalar_tensor_tensor(low[h][:, :, cols], above[:, :, cols], -1.0, gap[:, :, cols], ALU.mult, ALU.min)
+
+        def sum_by_transposes(blk):
+            cols = blocks[blk]
+            lift = sbuf("lift%d" % blk, [P, PACK, P], F32)
+            nc.scalar.activation(lift[:], low[0][:, :, cols], ACT.Relu, scale=-3.0)
+            turned = bank(blk)
+            for e in range(PACK):
+                terms = [hi[0][:, e, cols], low[0][:, e, cols], lift[:, e, :]]
+                for i, term in enumerate(terms):
+                    nc.tensor.matmul(
+                        turned[:, P * e : P * e + P], term, ident[:],
+                        start=(i == 0), stop=(i == len(terms) - 1), is_transpose=True,
+                    )
+            turned_sum = sbuf("turned_sum%d" % blk, [P, S], F32)
+            nc.scalar.copy(turned_sum[:], turned[:])
+            back = bank(3 + blk)
+            for e in range(PACK):
+                nc.tensor.transpose(back[:, P * e : P * e + P], turned_sum[:, P * e : P * e + P], ident[:])
+            nc.scalar.copy(out_first[:, :, cols], back[:].rearrange("p (e v) -> p e v", e=PACK))
+            woven = out_woven[0][:, PACK * P * blk : PACK * P * (blk + 1)]
+            nc.scalar.copy(woven.rearrange("p (v e) -> p v e", e=PACK), back[:].rearrange("p (e v) -> p v e", e=PACK))
+
+        for e in range(PACK):
+            look_up(c[:, e, :], s_win[e], list7, 0, S)
+        diff_first = half_tiles("diff", 0)
+        for e in range(PACK):
+            a_less_c(0, e, diff_first)
+        gap_first = gap_and_hi(0, diff_first, None)
+        above_first = b_less_hi(0)
+
+        diff_second = half_tiles("diff", 1)
+        for e in range(PACK):
+            a_less_c(1, e, diff_second)
+            if e < len(blocks):
+                lower(0, blocks[e], above_first, gap_first)
+                sum_by_transposes(e)
+        gap_second = gap_and_hi(1, diff_second, "lift0")
+        nc.sync.dma_start(out_rows[:, :, 0:HALF], out_first[:])
+        quantise(out_code[:].bitcast(U32), out_scale, 0, HALF, out_woven[0][:])
+        nc.sync.dma_start(out_words[:, 0:HALF], out_code[:, 0:HALF])
+        above_second = b_less_hi(1)
+
         for cols in blocks:
-            nc.vector.scalar_tensor_tensor(s["tt"][:, :, cols], s["pp"][:, :, cols], -1.0, s["au"][:, :, cols], ALU.mult, ALU.min)
+            lower(1, cols, above_second, gap_second)
+        rise = diff_second
         for cols in blocks:
-            nc.vector.scalar_tensor_tensor(s["u"][:, :, cols], s["tt"][:, :, cols], -2.0, s["tt"][:, :, cols], ALU.mult, ALU.max)
-        for b, cols in enumerate(blocks):
-            o = keep.tile([P, PACK, P], F32, name="o_1%d" % b, tag=["o_10", "ob_0"][b], align_bytes=64)
-            nc.vector.tensor_tensor(o[:], s["u"][:, :, cols], s["hi"][:, :, cols], ALU.add)
-            nc.sync.dma_start(out_rows[:, :, HALF + P * b : HALF + P * b + P], o[:])
-            weave([nc.scalar.copy, nc.vector.tensor_copy][b], ob[1][:, PACK * P * b : PACK * P * (b + 1)], o[:])
-        hand_on(1)
+            nc.vector.scalar_tensor_tensor(rise[:, :, cols], low[1][:, :, cols], -2.0, low[1][:, :, cols], ALU.mult, ALU.max)
+        for blk, cols in enumerate(blocks):
+            last = blk == len(blocks) - 1
+            out_block = sbuf("out_block%d" % blk, [P, PACK, P], F32, "out_woven0" if last else None)
+            nc.vector.tensor_tensor(out_block[:], rise[:, :, cols], hi[1][:, :, cols], ALU.add)
+            nc.sync.dma_start(out_rows[:, :, HALF + P * blk : HALF + P * (blk + 1)], out_block[:])
+            woven = out_woven[1][:, PACK * P * blk : PACK * P * (blk + 1)]
+            weave(nc.vector.tensor_copy if last else nc.scalar.copy, woven, out_block[:])
+        for blk in range(len(blocks)):
+            woven = out_woven[1][:, PACK * P * blk : PACK * P * (blk + 1)]
+            quantise(out_code[:].bitcast(U32), out_scale, HALF + P * blk, P, woven)
+        nc.scalar.dma_start(out_words[:, HALF:], out_code[:, HALF:])
         for q in range(4):
             queue = nc.sync if q % 2 == 0 else nc.scalar
-            queue.dma_start(out_2[0][4 * q : 4 * q + 4, :].bitcast(I32), osc[32 * q : 32 * q + 4, :].bitcast(I32))
+            queue.dma_start(out_2[0][4 * q : 4 * q + 4, :].bitcast(I32), out_scale[32 * q : 32 * q + 4, :].bitcast(I32))

from contextlib import ExitStack

import concourse.mybir as mybir
from concourse.masks import make_identity

F32 = mybir.dt.float32
BF16 = mybir.dt.bfloat16
I32 = mybir.dt.int32
U32 = mybir.dt.uint32
U16 = mybir.dt.uint16
U8 = mybir.dt.uint8
FP8X4 = mybir.dt.float8_e4m3fn_x4
FP4X4 = mybir.dt.float4_e2m1fn_x4
ALU = mybir.AluOpType
ACT = mybir.ActivationFunctionType

P = 128
TOKENS = 2048
S = 512
PACK = 4
HALF = S // 2
RUN = 8
LIST_ROWS = 16
HALF_SCORE_SCALE = 0.0625 / 2
FLOPS = 4 * 2 * 512 * 512 * 512


def tile_picked_twksoftbrmstop2_none_po_kernel(
    tc, x_words, x_scales, w1_words, w1_scales, w2_words, w2_scales, w3_words, w3_scales, ga, gb,
    offs, two, n1, n2, three, n3, n4, n5, n6, n7, out_0, out_1, out_2,
):
    nc = tc.nc
    with ExitStack() as ctx:
        keep = ctx.enter_context(tc.tile_pool(name="keep", bufs=1))
        psum = ctx.enter_context(tc.psum_pool(name="psum", bufs=1))

        def sbuf(name, shape, dtype, over=None):
            return keep.tile(shape, dtype, name=name, tag=over or name, align_bytes=64)

        def bank(number):
            return psum.tile([P, S], F32, name="bank%d" % number, tag="bank%d" % number)

        def planes(name, width=S, over=(None,) * PACK):
            return [sbuf("%s%d" % (name, t), [P, width], F32, over[t]) for t in range(PACK)]

        def load_list(name, src):
            tile = keep.tile([P, S // LIST_ROWS], U16, name=name)
            nc.sync.dma_start(tile[:], src)
            return tile

        def load_scale_rows(dst, src):
            for q in range(4):
                nc.sync.dma_start(dst[32 * q : 32 * q + 4, :], src[0][4 * q : 4 * q + 4, :].bitcast(I32))

        def look_up(out, window, offsets, lo, n, other=None, op=None):
            picked = window[:].indirect(offsets[:, lo // LIST_ROWS : (lo + n) // LIST_ROWS])
            if other is None:
                nc.vector.tensor_copy(out, picked)
            else:
                nc.vector.tensor_tensor(out, picked, other, op)

        def weave(copy, dst, src):
            copy(dst.rearrange("p (c i t) -> p c t i", i=4, t=PACK), src.rearrange("p t (c i) -> p c t i", i=4))

        x_scale = sbuf("x_scale", [P, TOKENS // 4], I32)
        nc.gpsimd.memset(x_scale[:], 0)
        w_scale = [sbuf("w_scale%d" % i, [P, S // 4], I32) for i in range(3)]
        w_code = [sbuf("w_code%d" % i, [P, S // 2], I32) for i in range(3)]
        w_words = [w2_words, w3_words, w1_words]
        w_scales = [w2_scales, w3_scales, w1_scales]
        gain_rows = sbuf("gain_rows", [P, P], F32)
        nc.gpsimd.memset(gain_rows[:], 0.0)
        quarter = sbuf("quarter", [P, 1], F32)
        nc.vector.memset(quarter[:], 0.25)
        for i in range(3):
            nc.vector.memset(w_scale[i][:], 0)
        for first_row, gain in ((0, ga), (PACK, gb)):
            nc.gpsimd.dma_start(
                gain_rows[first_row : first_row + PACK, :].rearrange("t (b r) -> t b r", r=RUN),
                gain.rearrange("(b t r) o -> t b (r o)", t=PACK, r=RUN),
            )
        ident = sbuf("ident", [P, P], F32)
        make_identity(nc, ident[:])

        x_code = sbuf("x_code", [P, TOKENS], I32)
        token_lists = [load_list("two", two), load_list("three", three), load_list("offs", offs)]
        load_scale_rows(x_scale, x_scales)
        nc.sync.dma_start(x_code[:], x_words[0].rearrange("p n t -> p (n t)").bitcast(I32))

        def load_weight(i):
            load_scale_rows(w_scale[i], w_scales[i])
            nc.sync.dma_start(w_code[i][:], w_words[i][0].bitcast(I32))

        load_weight(0)
        list2 = load_list("list2", n2)
        load_weight(1)
        load_weight(2)
        list3 = load_list("list3", n3)
        list1 = load_list("list1", n1)
        list4 = load_list("list4", n4)
        list7 = load_list("list7", n7)
        list5 = load_list("list5", n5)
        list6 = load_list("list6", n6)

        gain_bank = bank(7)
        nc.tensor.transpose(gain_bank[:, 0:P], gain_rows[:], ident[:])
        gain_cols = sbuf("gain_cols", [P, 2 * PACK], F32)
        nc.scalar.copy(gain_cols[:], gain_bank[:, 0 : 2 * PACK])

        picked_scale = [sbuf("picked_scale%d" % i, [P, S], U8) for i in range(3)]
        staging_taken = [None, "w_code0", "w_scale0"]
        picked_code = [sbuf("picked_code%d" % i, [P, S], U32, staging_taken[i]) for i in range(3)]
        dealt_code = [sbuf("dealt_code%d" % i, [P, S // 2], I32) for i in range(3)]
        dealt_scale = [sbuf("dealt_scale%d" % i, [P, S // 4], I32) for i in range(3)]

        def deal(dst, src, run_words):
            nc.vector.tensor_copy(
                dst[:].rearrange("p (t b w) -> p t b w", t=PACK, w=run_words),
                src[:].rearrange("p (b t w) -> p t b w", t=PACK, w=run_words),
            )

        for i in range(3):
            nc.vector.tensor_copy(picked_scale[i][:], x_scale[:].bitcast(U8).indirect(token_lists[i][:]))
        for i in range(3):
            nc.vector.tensor_copy(picked_code[i][:], x_code[:].bitcast(U32).indirect(token_lists[i][:]))
            deal(dealt_scale[i], w_scale[i], RUN // 4)
            deal(dealt_code[i], w_code[i], RUN // 2)

        def product(i, t, acc):
            code_words, scale_words = P // 2, P // 4
            nc.tensor.matmul_mx(
                out=acc[:],
                lhsT=dealt_code[i][:, code_words * t : code_words * (t + 1)].bitcast(U8).bitcast(FP4X4),
                lhsT_scale=dealt_scale[i][:, scale_words * t : scale_words * (t + 1)].bitcast(U8),
                rhs=picked_code[i][:].bitcast(FP8X4),
                rhs_scale=picked_scale[i][:],
                start=True,
                stop=True,
            )

        d_win = planes("d_win", 2 * S)
        sq_win = planes("sq_win", 2 * S, (None, "w_code1", None, "w_code2"))
        y_win = planes("y_win", 2 * S)
        tanh_last = sbuf("tanh_last", [P, S], F32)
        tanh_d = [d_win[t + 1][:, S:] for t in range(PACK - 1)] + [tanh_last[:]]
        nc.vector.memset(d_win[0][:, S:], 0.0)
        under_root = [w[:, S:] for w in y_win]
        b_win, sq_plain = planes("b_win"), planes("sq_plain")
        s_win = planes("s_win", 2 * S)
        inv_root = [w[:, S:] for w in s_win]
        d_term = [w[:, S:] for w in sq_win]

        d_banks = [bank(t) for t in range(PACK)]
        b_banks = [bank(PACK + t) for t in range(PACK)]
        for t in range(PACK):
            product(0, t, d_banks[t])
            nc.scalar.activation(tanh_d[t], d_banks[t][:], ACT.Tanh)
            nc.scalar.activation(d_win[t][:, 0:S], d_banks[t][:], ACT.Copy, scale=gain_cols[:, t : t + 1])
        for t in range(PACK):
            product(1, t, b_banks[t])
            nc.scalar.activation(sq_win[t][:, 0:S], b_banks[t][:], ACT.Square)
            nc.scalar.activation(sq_plain[t][:], b_banks[t][:], ACT.Square)
        y_banks = [bank(t) for t in range(PACK)]
        for t in range(PACK):
            product(2, t, y_banks[t])
            nc.scalar.activation(y_win[t][:, 0:S], y_banks[t][:], ACT.Copy, scale=gain_cols[:, t : t + 1])
        for t in range(PACK):
            nc.scalar.activation(b_win[t][:], b_banks[t][:], ACT.Copy, scale=gain_cols[:, PACK + t : PACK + t + 1])

        for t in range(PACK):
            look_up(d_term[t], d_win[t], list2, 0, S, tanh_d[t], ALU.mult)
        for t in range(PACK):
            look_up(under_root[t], sq_win[t], list3, 0, S, sq_plain[t][:], ALU.add)
            nc.scalar.activation(inv_root[t], under_root[t], ACT.Abs_reciprocal_sqrt, bias=quarter[:])
        z = sbuf("z", [P, PACK, S], F32)
        for t in range(PACK):
            look_up(z[:, t, :], y_win[t], list1, 0, S, d_term[t], ALU.subtract)
        z_woven = sbuf("z_woven", [P, PACK * S], BF16)
        nc.scalar.copy(
            z_woven[:].rearrange("p (e m t) -> p m e t", e=PACK, t=PACK),
            z[:].rearrange("p t (m e) -> p m e t", e=PACK),
        )
        z_code = sbuf("z_code", [P, S], U32)
        z_scale = sbuf("z_scale", [P, S], U8)
        z2_code = sbuf("z2_code", [P, S], U32)
        z2_scale = sbuf("z2_scale", [P, S], U8)
        s_banks = [bank(PACK + e) for e in range(PACK)]

        def z2_columns(lo, n, over):
            z2 = sbuf("z2_from%d" % lo, [P, PACK, n], F32, over)
            for t in range(PACK):
                look_up(z2[:, t, :], b_win[t], list4, lo, n, inv_root[t][:, lo : lo + n], ALU.mult)
            return z2

        def quantise(code, scale, lo, n, woven):
            nc.vector.quantize_mx(out=code[:, lo : lo + n].bitcast(FP8X4), scales=scale[:, lo : lo + n], in_=woven)

        def scores(lo, n):
            for e in range(PACK):
                nc.tensor.matmul_mx(
                    out=s_banks[e][:, lo : lo + n],
                    lhsT=z_code[:, P * e : P * e + P].bitcast(FP8X4),
                    lhsT_scale=z_scale[:, P * e : P * e + P],
                    rhs=z2_code[:, lo : lo + n].bitcast(FP8X4),
                    rhs_scale=z2_scale[:, lo : lo + n],
                    start=True,
                    stop=True,
                )
                nc.scalar.activation(s_win[e][:, lo : lo + n], s_banks[e][:, lo : lo + n], ACT.Copy, scale=HALF_SCORE_SCALE)

        z2_first = z2_columns(0, HALF, None)
        z2_woven_first = sbuf("z2_woven_first", [P, PACK * HALF], BF16)
        weave(nc.scalar.copy, z2_woven_first[:], z2_first[:])
        quantise(z_code, z_scale, 0, S, z_woven[:])
        z2_third_quarter = z2_columns(HALF, P, "z_woven")
        z2_woven_second = sbuf("z2_woven_second", [P, PACK * HALF], BF16)
        weave(nc.scalar.copy, z2_woven_second[:, 0 : PACK * P], z2_third_quarter[:])
        quantise(z2_code, z2_scale, 0, HALF, z2_woven_first[:])
        scores(0, HALF)
        z2_last_quarter = z2_columns(HALF + P, P, "z2_woven_first")
        weave(nc.vector.tensor_copy, z2_woven_second[:, PACK * P :], z2_last_quarter[:])
        for blk in range(2):
            quantise(z2_code, z2_scale, HALF + P * blk, P, z2_woven_second[:, PACK * P * blk : PACK * P * (blk + 1)])
        scores(HALF, HALF)

        out_code = sbuf("out_code", [P, S], I32)
        out_scale = sbuf("out_scale", [P, S], U8)
        out_rows = out_0.rearrange("(p e) v -> p e v", e=PACK)
        out_words = out_1[0].rearrange("p n t -> p (n t)").bitcast(I32)
        blocks = [slice(0, P), slice(P, HALF)]

        def half_tiles(name, h, over=None):
            return sbuf("%s%d" % (name, h), [P, PACK, HALF], F32, over)

        hi, low = zip(*[(half_tiles("hi", h), half_tiles("low", h)) for h in range(2)])
        out_first = half_tiles("out_half", 0)
        out_woven = [sbuf("out_woven%d" % h, [P, PACK * HALF], BF16) for h in range(2)]
        c = sbuf("c", [P, PACK, S], F32)

        def a_less_c(h, e, diff):
            look_up(diff[:, e, :], s_win[e], list5, HALF * h, HALF, c[:, e, HALF * h : HALF * (h + 1)], ALU.subtract)

        def gap_and_hi(h, diff, over):
            gap = half_tiles("gap", h, over)
            for first in (0, 2):
                two_planes = slice(first, first + 2)
                nc.scalar.activation(
                    gap[:, two_planes, :].rearrange("p e v -> p (e v)"),
                    diff[:, two_planes, :].rearrange("p e v -> p (e v)"),
                    ACT.Abs,
                )
                nc.vector.scalar_tensor_tensor(
                    hi[h][:, two_planes, :], diff[:, two_planes, :], 0.0,
                    c[:, two_planes, HALF * h : HALF * (h + 1)], ALU.max, ALU.add,
                )
            return gap

        def b_less_hi(h):
            above = half_tiles("above", h)
            for e in range(PACK):
                look_up(above[:, e, :], s_win[e], list6, HALF * h, HALF, hi[h][:, e, :], ALU.subtract)
            return above

        def lower(h, cols, above, gap):
            nc.vector.scalar_tensor_tensor(low[h][:, :, cols], above[:, :, cols], -1.0, gap[:, :, cols], ALU.mult, ALU.min)

        def sum_by_transposes(blk):
            cols = blocks[blk]
            lift = sbuf("lift%d" % blk, [P, PACK, P], F32)
            nc.scalar.activation(lift[:], low[0][:, :, cols], ACT.Relu, scale=-3.0)
            turned = bank(blk)
            for e in range(PACK):
                terms = [hi[0][:, e, cols], low[0][:, e, cols], lift[:, e, :]]
                for i, term in enumerate(terms):
                    nc.tensor.matmul(
                        turned[:, P * e : P * e + P], term, ident[:],
                        start=(i == 0), stop=(i == len(terms) - 1), is_transpose=True,
                    )
            turned_sum = sbuf("turned_sum%d" % blk, [P, S], F32)
            nc.scalar.copy(turned_sum[:], turned[:])
            back = bank(3 + blk)
            for e in range(PACK):
                nc.tensor.transpose(back[:, P * e : P * e + P], turned_sum[:, P * e : P * e + P], ident[:])
            nc.scalar.copy(out_first[:, :, cols], back[:].rearrange("p (e v) -> p e v", e=PACK))
            woven = out_woven[0][:, PACK * P * blk : PACK * P * (blk + 1)]
            nc.scalar.copy(woven.rearrange("p (v e) -> p v e", e=PACK), back[:].rearrange("p (e v) -> p v e", e=PACK))

        for e in range(PACK):
            look_up(c[:, e, :], s_win[e], list7, 0, S)
        diff_first = half_tiles("diff", 0)
        for e in range(PACK):
            a_less_c(0, e, diff_first)
        gap_first = gap_and_hi(0, diff_first, None)
        above_first = b_less_hi(0)

        diff_second = half_tiles("diff", 1)
        for e in range(PACK):
            a_less_c(1, e, diff_second)
            if e < len(blocks):
                lower(0, blocks[e], above_first, gap_first)
                sum_by_transposes(e)
        gap_second = gap_and_hi(1, diff_second, "lift0")
        nc.sync.dma_start(out_rows[:, :, 0:HALF], out_first[:])
        quantise(out_code[:].bitcast(U32), out_scale, 0, HALF, out_woven[0][:])
        nc.sync.dma_start(out_words[:, 0:HALF], out_code[:, 0:HALF])
        above_second = b_less_hi(1)

        for cols in blocks:
            lower(1, cols, above_second, gap_second)
        rise = diff_second
        for cols in blocks:
            nc.vector.scalar_tensor_tensor(rise[:, :, cols], low[1][:, :, cols], -2.0, low[1][:, :, cols], ALU.mult, ALU.max)
        for blk, cols in enumerate(blocks):
            last = blk == len(blocks) - 1
            out_block = sbuf("out_block%d" % blk, [P, PACK, P], F32, "out_woven0" if last else None)
            nc.vector.tensor_tensor(out_block[:], rise[:, :, cols], hi[1][:, :, cols], ALU.add)
            nc.sync.dma_start(out_rows[:, :, HALF + P * blk : HALF + P * (blk + 1)], out_block[:])
            woven = out_woven[1][:, PACK * P * blk : PACK * P * (blk + 1)]
            weave(nc.vector.tensor_copy if last else nc.scalar.copy, woven, out_block[:])
        for blk in range(len(blocks)):
            woven = out_woven[1][:, PACK * P * blk : PACK * P * (blk + 1)]
            quantise(out_code[:].bitcast(U32), out_scale, HALF + P * blk, P, woven)
        nc.scalar.dma_start(out_words[:, HALF:], out_code[:, HALF:])
        for q in range(4):
            queue = nc.sync if q % 2 == 0 else nc.scalar
            queue.dma_start(out_2[0][4 * q : 4 * q + 4, :].bitcast(I32), out_scale[32 * q : 32 * q + 4, :].bitcast(I32))
